import numpy as np, ml_dtypes
CORES = [36,164,52,180,100,228,116,244]
N = 8
import mx_ref
BF = ml_dtypes.bfloat16
def entries(a):
    return np.ascontiguousarray(a.T).reshape(-1)
def table(e):
    return np.ascontiguousarray(np.reshape(e, (-1, 16)).T).astype(np.int32)
def gentries(a):
    return np.ascontiguousarray(a.reshape(8, 16, -1).transpose(0, 2, 1)).reshape(8, -1)
def gtable(e):
    e = np.asarray(e); return np.ascontiguousarray(e.reshape(8, -1, 16).transpose(0, 2, 1)).reshape(128, -1).astype(np.int32)
def tile(rs):
    return np.stack(rs, axis=2).reshape(128, -1).astype(BF)
def cut(t, i, w=512):
    return t[:, w * i:w * i + w]
def f(rng, *shape):
    return mx_ref.flush((rng.standard_normal(shape, dtype=np.float32) * np.exp2(rng.integers(-2, 3, shape[:-1] + (1,)))).astype(BF))
def wide(rng, *shape, cols=0):
    v = rng.standard_normal(shape, dtype=np.float32) * np.exp2(rng.integers(-12, 13, shape)).astype(np.float32)
    if cols: v *= np.repeat(np.exp2(rng.integers(-cols, cols + 1, shape[:-2] + (1, shape[-1] // 4))) * (rng.random(shape[:-2] + (1, shape[-1] // 4)) > 0.0625), 4, axis=-1).astype(np.float32)
    return mx_ref.flush(v.astype(BF))
T, CAPP, P = 256, 48, 256
SL = N * CAPP
G = 8
def pieces(rng, how):
    if how == "ones": n = np.ones((G, SL), int)
    elif how == "full":
        n = T - rng.integers(0, 8, (G, SL)); n[:, ::4] = T
    elif how == "powers":
        k = [1 << i for i in range(T.bit_length())]; k = sorted(set(k + [i + 1 for i in k if i < T]))
        n = rng.permuted(np.tile(np.resize(k, SL), (G, 1)), axis=1)
    else: n = np.where(rng.random((G, SL)) < 0.5, rng.integers(1, T + 1, (G, SL)), np.clip(np.exp2(rng.uniform(0, T.bit_length() - 1, (G, SL))).astype(int), 1, T))
    s = rng.integers(0, T - n + 1)
    if how == "full": s[:] = 0
    if how == "nested":
        for g in range(G):
            for r in range(N):
                m = rng.integers(0, T)
                b = np.sort(rng.choice(rng.integers(0, m + 1, 16), CAPP)); e = np.sort(rng.choice(rng.integers(m, T, 16), CAPP))[::-1]
                k = r * CAPP + rng.permutation(CAPP); s[g, k] = b; n[g, k] = e - b + 1
    return s, n
def lists(rng, how="any", every=False):
    held = np.zeros((N, N, CAPP), bool)
    for r in range(N):
        n = rng.integers(0, CAPP + 1, N); n[(r + rng.integers(1, N)) % N] = CAPP
        for q in range(N): held[q, r, rng.permutation(CAPP)[:CAPP if every else n[q]]] = True
    d = {"lo": [], "ln": [], "pf": [], "pg": []}
    for q in range(N):
        s, n = pieces(rng, how); e = ~held[q].reshape(-1)
        s[:, e] = -1; n[:, e] = 0
        d["lo"].append(gtable(s)); d["ln"].append(gtable(n))
    who = rng.permutation(N)
    for r in range(N):
        k = rng.permutation(np.flatnonzero(held[:, r]))
        first = rng.permutation(np.resize(k, P))
        second = np.where(rng.random(P) < 0.25, -1, rng.choice(k, P))
        if how == "ones":
            if r == who[0]:
                first[rng.permutation(P)[:P // 2]] = k[0]; second[rng.permutation(P)[:P // 2]] = k[0]
            if r == who[1]: second[:] = -1
            if r == who[2]: second = rng.choice(k, P)
        d["pf"].append(table(first))
        d["pg"].append(table(second))
    return {k: np.stack(t) for k, t in d.items()}
def setup_inputs(rng):
    return {"x": f(rng, N, 128, 4 * T), "a": f(rng, N, 128, 2048), "u": f(rng, N, 128, 512), "v": f(rng, N, 128, 512), **lists(rng)}
def setup_inputs_ones(rng):
    return {**setup_inputs(rng), **lists(rng, "ones")}
def setup_inputs_full(rng):
    return {**setup_inputs(rng), **lists(rng, "full", True)}
def setup_inputs_powers(rng):
    return {**setup_inputs(rng), **lists(rng, "powers", True)}
def setup_inputs_nested(rng):
    return {**setup_inputs(rng), **lists(rng, "nested", True)}
def setup_inputs_spread(rng):
    d = setup_inputs(rng); d["x"] = wide(rng, N, 128, 4 * T, cols=8); return d
def check_inputs(d):
    b = []; held = []
    for q in range(N):
        s, n = gentries(d["lo"][q]).reshape(G, -1), gentries(d["ln"][q]).reshape(G, -1)
        e = s == -1; held.append(~e[0])
        if s.min() < -1 or s.max() >= T or (e != e[:1]).any(): b.append("lo")
        if (n[e] != 0).any() or (n[~e] < 1).any() or (n[~e] > T - s[~e]).any(): b.append("ln")
    for r in range(N):
        h = np.concatenate([held[q][r * CAPP:r * CAPP + CAPP] for q in range(N)])
        for k, least in (("pf", 0), ("pg", -1)):
            j = entries(d[k][r])
            if j.min() < least or j.max() >= SL or not h[j[(j >= 0) & (j < SL)]].all(): b.append(k)
    return b
def reference(x, a, u, v, lo, ln, pf, pg):
    sent = []
    for q in range(N):
        X = mx_ref.quantize(x[q])
        Z = np.stack([mx_ref.matmul(mx_ref.quantize(np.ascontiguousarray(cut(a[q], i))), X) for i in range(4)])
        h = np.maximum(Z, np.float32(0)) * np.float32(0.05)
        s, n = gentries(lo[q]), gentries(ln[q])
        R = np.zeros((4, 128, SL), np.float32)
        for k in range(SL):
            for g in range(8):
                if n[g, k]: R[:, 16 * g:16 * g + 16, k] = h[:, 16 * g:16 * g + 16, s[g, k]:s[g, k] + n[g, k]].max(axis=2)
        sent.append([mx_ref.quantize(np.ascontiguousarray(tile([R[i][:, CAPP * r:CAPP * r + CAPP] for i in range(4)]))) for r in range(N)])
    y = np.zeros((N, 128, P), np.float32)
    for r in range(N):
        V, U = mx_ref.quantize(v[r]), mx_ref.quantize(u[r])
        zv = np.concatenate([mx_ref.matmul(V, sent[q][r]) for q in range(N)], axis=1)
        zu = np.concatenate([mx_ref.matmul(U, sent[q][r]) for q in range(N)], axis=1)
        first, second = entries(pf[r]), entries(pg[r])
        y[r] = zv[:, first]
        two = second >= 0
        y[r][:, two] += zu[:, second[two]]
    return {"y": y}

@@ -1,0 +1,339 @@
+from concourse.bass import DstId, RemoteDMATransfer
+from concourse.mybir import dt, AluOpType, ActivationFunctionType
+
+N, CAPP, COLS, P = 8, 48, 256, 256
+SL = N * CAPP
+LW = SL // 16
+LAND = (N - 1) * CAPP
+AT = (0, 4 * CAPP, 6 * CAPP, 8 * CAPP)
+RUN = 128
+LEV = 7
+BY_S, BY_G = (1, 2), (3,)
+PACKED = BY_S + BY_G
+ZW = 392
+
+
+def width(k):
+    return COLS // 2 if k in PACKED else COLS - (1 << k)
+
+
+def layout():
+    b, f, m, at, am = {}, {}, {}, 2 + COLS, 0
+    for k in range(1, LEV + 1):
+        b[k], f[k], m[k] = at, at + width(k), am
+        at, am = at + 2 * width(k), am + width(k)
+    return b, f, m, at, am
+
+
+BK, FK, MK, TW, MW = layout()
+TS = (TW + 15) // 16 * 16
+
+SCRATCH = {
+    "lol": ("sbuf", [128, 2 * LW], "int32"),
+    "lr": ("sbuf", [128, 2 * LW], "float32"),
+    "tj": ("sbuf", [128, 16 * LW], "bfloat16"),
+    "dif": ("sbuf", [128, 8 * LW], "float32"),
+    "cb": ("sbuf", [128, 8 * LW], "float32"),
+    "cf": ("sbuf", [128, 8 * LW], "float32"),
+    "pb": ("sbuf", [128, 8 * LW], "float32"),
+    "pq": ("sbuf", [128, 8 * LW], "float32"),
+    "offl": ("sbuf", [128, LW], "uint16"),
+    "offr": ("sbuf", [128, LW], "uint16"),
+    "xt": ("sbuf", [128, 1024], "bfloat16"),
+    "at": ("sbuf", [128, 2048], "bfloat16"),
+    "uvt": ("sbuf", [128, 1024], "bfloat16"),
+    "qx": ("sbuf", [128, 256], "float8_e4m3fn_x4"),
+    "sx": ("sbuf", [128, 256], "uint8"),
+    "qa": ("sbuf", [128, 512], "float8_e4m3fn_x4"),
+    "sa": ("sbuf", [128, 512], "uint8"),
+    "quv": ("sbuf", [128, 256], "float8_e4m3fn_x4"),
+    "suv": ("sbuf", [128, 256], "uint8"),
+    "h0": ("sbuf", [128, 4, 4, 4, 4], "bfloat16"),
+    "h1": ("sbuf", [128, 4, 4, 4, 4], "bfloat16"),
+    "h2": ("sbuf", [128, 4, 4, 4, 4], "bfloat16"),
+    "h3": ("sbuf", [128, 4, 4, 4, 4], "bfloat16"),
+    "tab": ("sbuf", [128, 4 * TS], "bfloat16"),
+    "mask": ("sbuf", [128, MW], "bfloat16"),
+    "pk": ("sbuf", [128, 4 * len(PACKED) * COLS], "bfloat16"),
+    "left": ("sbuf", [128, 4 * SL], "bfloat16"),
+    "pt": ("sbuf", [128, 4 * SL], "bfloat16"),
+    "q0": ("sbuf", [128, 4 * CAPP], "float8_e4m3fn_x4"),
+    "s0": ("sbuf", [128, 4 * CAPP], "uint8"),
+    "q1": ("sbuf", [128, RUN], "float8_e4m3fn_x4"),
+    "s1": ("sbuf", [128, RUN], "uint8"),
+    "q2": ("sbuf", [128, RUN], "float8_e4m3fn_x4"),
+    "s2": ("sbuf", [128, RUN], "uint8"),
+    "lc": ("sbuf", [128, LAND], "float8_e4m3fn_x4"),
+    "ls": ("sbuf", [128, LAND], "uint8"),
+    "lp": ("sbuf", [128, 32], "int32"),
+    "offp": ("sbuf", [128, 32], "uint16"),
+    "zv": ("sbuf", [128, ZW], "float32"),
+    "zu": ("sbuf", [128, ZW], "float32"),
+    "first": ("sbuf", [128, P], "float32"),
+    "yt": ("sbuf", [128, P], "float32"),
+    "ps": ("psum", [128, 4096], "float32"),
+}
+SEMAPHORES = ["vs", "ss", "ts", "gs", "lst", "lx", "la0", "la1", "la2", "la3", "luv", "lpl", "got0", "got1", "got2", "sent",
+              "st0", "st1"]
+
+
+def half(h, k, bit):
+    ix = [slice(None)] * 5
+    ix[4 - k // 2] = slice(2 * bit, 2 * bit + 2) if k % 2 else slice(bit, None, 2)
+    return h[tuple(ix)]
+
+
+def falling(buf, a, w):
+    return buf[:, a + w - 1:(a - 1 if a else None):-1]
+
+
+def groups(rank):
+    h, p = rank // 4, rank // 2
+    return 4 * (1 - h), 2 * (p ^ 1), 2 * p
+
+
+def rank_program(g, core, T, topo):
+    rank = T.rank_of(core)
+    if rank is None:
+        return
+    V, S, PE, Y = g.vector, g.scalar, g.tensor, g.sync
+    A, F = AluOpType, ActivationFunctionType
+    vs, ss, ts, gs = T.sem.vs, T.sem.ss, T.sem.ts, T.sem.gs
+    group = groups(rank)
+    n = {"v": 0, "s": 0, "t": 0, "g": 0}
+
+    def v(i):
+        n["v"] += 1
+        i.then_inc(vs, 1)
+        return n["v"]
+
+    def s(i):
+        n["s"] += 1
+        i.then_inc(ss, 1)
+        return n["s"]
+
+    def t(i):
+        n["t"] += 1
+        i.then_inc(ts, 1)
+        return n["t"]
+
+    def gp(i):
+        n["g"] += 1
+        i.then_inc(gs, 1)
+        return n["g"]
+
+    def bank(b, w):
+        return T.ps[:, 512 * b:512 * b + w]
+
+    S.dma_start(T.lol[:, 0:LW], T.lo[:]).then_inc(T.sem.lst, 16)
+    S.dma_start(T.lol[:, LW:2 * LW], T.ln[:]).then_inc(T.sem.lst, 16)
+    Y.dma_start(T.xt[:], T.x[:]).then_inc(T.sem.lx, 16)
+    for i in range(4):
+        Y.dma_start(T["at"][:, 512 * i:512 * i + 512], T.a[:, 512 * i:512 * i + 512]).then_inc(T.sem["la%d" % i], 16)
+    Y.dma_start(T.uvt[:, 0:512], T.u[:]).then_inc(T.sem.luv, 16)
+    Y.dma_start(T.uvt[:, 512:1024], T.v[:]).then_inc(T.sem.luv, 16)
+    for k in range(8):
+        Y.dma_start(T.lp[16 * k:16 * k + 16, 0:16], T.pf[:]).then_inc(T.sem.lpl, 16)
+        Y.dma_start(T.lp[16 * k:16 * k + 16, 16:32], T.pg[:]).then_inc(T.sem.lpl, 16)
+
+    ones = v(V.memset(T.mask[:], 1.0))
+    v(V.memset(T.tj[:, 0::8], 0.0))
+    v(V.memset(T.cb[:, 7::8], 0.0))
+    v(V.memset(T.cf[:, 7::8], 0.0))
+    v(V.memset(T.tab[:, 0::TS], 0.0))
+    v(V.memset(T.tab[:, 1 + COLS::TS], 0.0))
+    for k in range(1, LEV + 1):
+        if k not in PACKED:
+            v(V.memset(T.cb[:, 7 - k::8], BK[k] - 1.0))
+            v(V.memset(T.cf[:, 7 - k::8], FK[k] - (1 << k) - 1.0))
+
+    V.wait_ge(T.sem.lst, 32)
+    v(V.tensor_scalar(T.lr[:, 0:LW], T.lol[:, 0:LW], 1, None, A.add))
+    lists = v(V.tensor_tensor(T.lr[:, LW:2 * LW], T.lol[:, 0:LW], T.lol[:, LW:2 * LW], A.add))
+    V.wait_ge(vs, ones)
+    for k in range(1, LEV + 1):
+        consts = v(V.memset(T.mask[:, MK[k]:MK[k] + width(k):1 << k], 0.0))
+
+    S.wait_ge(vs, lists)
+    for j in range(LEV, 0, -1):
+        floors = s(S.activation(T.tj[:, 8 - j::8], T.lr[:], F.Identity, bias=128.5 - 2.0 ** -(j + 1), scale=2.0 ** -j))
+    S.wait_ge(ss, floors)
+    for j in PACKED:
+        w = 2.0 ** (j - 1)
+        s(S.activation(T.cb[:, 7 - j::8], T.tj[:, 8 * LW + 8 - j::8], F.Identity, bias=BK[j] - 1 + w + 129 * w, scale=-w))
+        cands = s(S.activation(T.cf[:, 7 - j::8], T.tj[:, 8 * LW + 8 - j::8], F.Identity, bias=FK[j] - 1 - w + 129 * w, scale=-w))
+
+    def product_a(i):
+        V.wait_ge(T.sem["la%d" % i], 16)
+        c = slice(128 * i, 128 * i + 128)
+        q = v(V.quantize_mx(T.qa[:, c], T.sa[:, c], T["at"][:, 512 * i:512 * i + 512]))
+        PE.wait_ge(vs, q)
+        return t(PE.matmul_mx(bank(i, COLS), T.qa[:, c], T.sa[:, c], T.qx[:], T.sx[:], True, True))
+
+    def packed(i, k, bit):
+        return COLS * (len(PACKED) * i + PACKED.index(k)) + 128 * bit
+
+    def result(i, z):
+        S.wait_ge(ts, z)
+        r = s(S.activation(T.tab[:, TS * i + 1:TS * i + 1 + COLS], bank(i, COLS), F.Relu, scale=0.05))
+        return r, s(S.activation(T["h%d" % i][:], bank(i, COLS), F.Relu, scale=0.05))
+
+    def pack(i, r):
+        h = T["h%d" % i]
+        S.wait_ge(ss, r[1])
+        g.wait_ge(ss, r[1])
+        ready = {}
+        for k in PACKED:
+            for bit in (0, 1):
+                a = packed(i, k, bit)
+                if k in BY_S:
+                    ready[k] = (ss, s(S.activation(T.pk[:, a:a + 128], half(h, k, bit), F.Copy)))
+                else:
+                    ready[k] = (gs, gp(g.affine_select(T.pk[:, a:a + 128], half(h, k, bit), [[0, 128]], A.is_equal, 0.0, 0, 0)))
+        return ready
+
+    def scans(i, k, fall, rise):
+        w = width(k)
+        m = T.mask[:, MK[k]:MK[k] + w]
+        v(V.tensor_tensor_scan(falling(T.tab, TS * i + BK[k], w), m, fall, 0.0, A.mult, A.max))
+        return v(V.tensor_tensor_scan(T.tab[:, TS * i + FK[k]:TS * i + FK[k] + w], m, rise, 0.0, A.mult, A.max))
+
+    def high(i, r):
+        V.wait_ge(ss, r[0])
+        V.wait_ge(vs, consts)
+        for k in range(LEV, 0, -1):
+            if k not in PACKED:
+                w, h0 = width(k), TS * i + 1
+                scans(i, k, falling(T.tab, h0, w), T.tab[:, h0 + COLS - w:h0 + COLS])
+
+    def low(i, ready):
+        for k in PACKED:
+            V.wait_ge(*ready[k])
+            a, b = packed(i, k, 0), packed(i, k, 1)
+            last = scans(i, k, falling(T.pk, a, 128), T.pk[:, b:b + 128])
+        return last
+
+    V.wait_ge(T.sem.lx, 16)
+    v(V.quantize_mx(T.qx[:], T.sx[:], T.xt[:]))
+    V.wait_ge(ss, floors)
+    d = v(V.tensor_tensor(T.dif[:], T.tj[:, 8 * LW:16 * LW], T.tj[:, 0:8 * LW], A.is_gt))
+    z0 = product_a(0)
+    V.wait_ge(ss, cands)
+    V.wait_ge(vs, d)
+    b = v(V.tensor_tensor_scan(T.pb[:], T.dif[:], T.cb[:], 0.0, A.mult, A.max))
+    f = v(V.tensor_tensor_scan(T.pq[:], T.dif[:], T.cf[:], 0.0, A.mult, A.max))
+    V.wait_ge(vs, b)
+    v(V.tensor_tensor(T.offl[:], T.pb[:, 7::8], T.lr[:, 0:LW], A.add))
+    V.wait_ge(vs, f)
+    offs = v(V.tensor_tensor(T.offr[:], T.pq[:, 7::8], T.lr[:, LW:2 * LW], A.add))
+    z1 = product_a(1)
+    r0 = result(0, z0)
+    r1 = result(1, z1)
+    p0 = pack(0, r0)
+    p1 = pack(1, r1)
+    high(0, r0)
+    r2 = result(2, product_a(2))
+    p2 = pack(2, r2)
+    high(1, r1)
+    w0 = low(0, p0)
+    r3 = result(3, product_a(3))
+    p3 = pack(3, r3)
+    high(2, r2)
+    w1 = low(1, p1)
+    high(3, r3)
+    w2 = low(2, p2)
+    w3 = low(3, p3)
+
+    def left(j):
+        k, w, o = AT[j], AT[j + 1] - AT[j], CAPP * group[j] // 16
+        done = []
+        for i, c in enumerate((w0, w1, w2, w3)):
+            S.wait_ge(vs, max(c, offs))
+            done.append(s(S.activation(T.left[:, SL * i + k:SL * i + k + w],
+                                       T.tab[:, TS * i:TS * i + TW].indirect(T.offl[:, o:o + w // 16]), F.Copy)))
+        return done
+
+    def right(j, lefts):
+        k, w, o = AT[j], AT[j + 1] - AT[j], CAPP * group[j] // 16
+        V.wait_ge(vs, offs)
+        for i in range(4):
+            V.wait_ge(ss, lefts[i])
+            full = v(V.tensor_tensor(T.pt[:, 4 * k + i:4 * (k + w):4],
+                                     T.tab[:, TS * i:TS * i + TW].indirect(T.offr[:, o:o + w // 16]),
+                                     T.left[:, SL * i + k:SL * i + k + w], A.max))
+        V.wait_ge(vs, full)
+        w = max(w, RUN)
+        return v(V.quantize_mx(T["q%d" % j][:], T["s%d" % j][:], T.pt[:, 4 * (AT[j + 1] - w):4 * AT[j + 1]]))
+
+    def send(j, q):
+        to = [r for r in range(group[j], group[j] + (AT[j + 1] - AT[j]) // CAPP) if r != rank]
+        first = RUN - 2 * CAPP if j else 0
+        g.wait_ge(vs, q)
+        for src, dst, codes in (("q%d" % j, "lc", True), ("s%d" % j, "ls", False)):
+            tr = []
+            for i, r in enumerate(to):
+                d = T.cores[r]
+                rid, pid = topo.addr(d, core)
+                at = AT[j] + CAPP * (rank - groups(r)[j] if j < 2 else 0)
+                c = first + CAPP * (r - group[j])
+                a, b = T[src][:, c:c + CAPP], T[dst][:, at:at + CAPP]
+                if codes:
+                    a, b = a.bitcast(dt.uint8), b.bitcast(dt.uint8)
+                e = topo.engines(core, d)
+                w = len(e) // len(to)
+                tr.append(RemoteDMATransfer(dst_ids=[DstId(rid=rid, pnc=pid)], dma_engine_mask=sum(1 << x for x in e[w * i:w * i + w]),
+                                            remote_sem=T.sem["got%d" % j], src=a, dst=b))
+            g.remote_dma_fused(tr, local_sem=T.sem.sent)
+        return 2 * w * len(to)
+
+    lefts = [left(j) for j in range(3)]
+    sent = 0
+    for j in range(3):
+        last = right(j, lefts[j])
+        sent = sent + send(j, last)
+
+    V.wait_ge(T.sem.luv, 32)
+    quv = v(V.quantize_mx(T.quv[:], T.suv[:], T.uvt[:]))
+    v(V.memset(T.zv[:, 0:1], 0.0))
+    v(V.memset(T.zu[:, 0:1], 0.0))
+    V.wait_ge(T.sem.lpl, 256)
+    places = v(V.tensor_scalar(T.offp[:], T.lp[:], 1, None, A.add))
+
+    def products(bv, codes, scales, a, b, lo, hi, slot):
+        for bk, c0 in ((bv, 128), (bv + 1, 0)):
+            z = t(PE.matmul_mx(bank(bk, b - a), T.quv[:, c0:c0 + 128], T.suv[:, c0:c0 + 128], codes[:, a:b], scales[:, a:b], True, True))
+            src = T.ps[:, 512 * bk + lo - a:512 * bk + hi - a]
+            if c0:
+                S.wait_ge(ts, z)
+                cv = s(S.activation(T.zv[:, 1 + slot:1 + slot + hi - lo], src, F.Copy))
+            else:
+                V.wait_ge(ts, z)
+                cu = v(V.tensor_copy(T.zu[:, 1 + slot:1 + slot + hi - lo], src))
+        return cv, cu
+
+    own = RUN - 2 * CAPP + CAPP * (rank - group[2])
+    PE.wait_ge(vs, quv)
+    PE.wait_ge(ss, lefts[2][3])
+    products(4, T.q2, T.s2, 0, RUN, own, own + CAPP, CAPP * rank)
+    for j, bk in ((0, 6), (1, 0), (2, 2)):
+        end = AT[j + 1] if j < 2 else LAND
+        PE.wait_ge(T.sem["got%d" % j], 16)
+        slot = CAPP * (group[j] if j < 2 else rank ^ 1)
+        cv, cu = products(bk, T.lc, T.ls, end - max(end - AT[j], RUN), end, AT[j], end, slot)
+
+    S.wait_ge(vs, places)
+    S.wait_ge(ss, cv)
+    V.wait_ge(vs, cu)
+    done = []
+    for k in range(2):
+        c = slice(128 * k, 128 * k + 128)
+        f = s(S.activation(T.first[:, c], T.zv[:, 0:1 + SL].indirect(T.offp[:, 8 * k:8 * k + 8]), F.Copy))
+        V.wait_ge(ss, f)
+        done.append(v(V.tensor_tensor(T.yt[:, c], T.zu[:, 0:1 + SL].indirect(T.offp[:, 16 + 8 * k:24 + 8 * k]), T.first[:, c], A.add)))
+    Y.wait_ge(vs, done[0])
+    Y.dma_start(T.y[:, 0:128], T.yt[:, 0:128]).then_inc(T.sem.st0, 16)
+    S.wait_ge(vs, done[1])
+    S.dma_start(T.y[:, 128:256], T.yt[:, 128:256]).then_inc(T.sem.st1, 16)
+    g.wait_ge(T.sem.sent, sent)
+    Y.wait_ge(T.sem.st0, 16)
+    S.wait_ge(T.sem.st1, 16)

@@ -5,40 +5,40 @@ N, CAPP, COLS, P = 8, 48, 256, 256
 SL = N * CAPP
 LW = SL // 16
 LAND = (N - 1) * CAPP
-AT = (0, 4 * CAPP, 6 * CAPP, 8 * CAPP)
 RUN = 128
-LEV = 7
-BY_S, BY_G = (1, 2), (3,)
-PACKED = BY_S + BY_G
+PW = 448
+LOW, TOP = 2, 7
+PL = TOP - LOW + 1
+PACK = {(4, 0): "s", (4, 1): "s", (5, 0): "s", (3, 0): "g", (3, 1): "g"}
 ZW = 392
 
 
-def width(k):
-    return COLS // 2 if k in PACKED else COLS - (1 << k)
+def width(k, side):
+    return COLS // 2 if (k, side) in PACK else COLS if k == LOW else COLS - (1 << k)
 
 
 def layout():
-    b, f, m, at, am = {}, {}, {}, 2 + COLS, 0
-    for k in range(1, LEV + 1):
-        b[k], f[k], m[k] = at, at + width(k), am
-        at, am = at + 2 * width(k), am + width(k)
-    return b, f, m, at, am
+    tb, m, at, am = {}, {}, 2 + COLS, 0
+    for k in range(LOW, TOP + 1):
+        tb[k, 0], tb[k, 1], m[k] = at, at + width(k, 0), am
+        at, am = at + width(k, 0) + width(k, 1), am + max(width(k, 0), width(k, 1))
+    return tb, m, at, am
 
 
-BK, FK, MK, TW, MW = layout()
+TB, MK, TW, MW = layout()
 TS = (TW + 15) // 16 * 16
 
 SCRATCH = {
     "lol": ("sbuf", [128, 2 * LW], "int32"),
-    "lr": ("sbuf", [128, 2 * LW], "float32"),
-    "tj": ("sbuf", [128, 16 * LW], "bfloat16"),
-    "dif": ("sbuf", [128, 8 * LW], "float32"),
-    "cb": ("sbuf", [128, 8 * LW], "float32"),
-    "cf": ("sbuf", [128, 8 * LW], "float32"),
-    "pb": ("sbuf", [128, 8 * LW], "float32"),
-    "pq": ("sbuf", [128, 8 * LW], "float32"),
-    "offl": ("sbuf", [128, LW], "uint16"),
-    "offr": ("sbuf", [128, LW], "uint16"),
+    "lr": ("sbuf", [128, 3 * LW], "float32"),
+    "tj": ("sbuf", [128, 2 * PL * LW], "bfloat16"),
+    "edge": ("sbuf", [128, 4 * LW], "bfloat16"),
+    "dif": ("sbuf", [128, PL * LW], "bfloat16"),
+    "dlow": ("sbuf", [128, 2 * LW], "bfloat16"),
+    "cand": ("sbuf", [128, 2 * PL * LW], "float32"),
+    "pick": ("sbuf", [128, 2 * PL * LW], "float32"),
+    "base": ("sbuf", [128, 2 * LW], "float32"),
+    "off": ("sbuf", [128, 2 * LW], "uint16"),
     "xt": ("sbuf", [128, 1024], "bfloat16"),
     "at": ("sbuf", [128, 2048], "bfloat16"),
     "uvt": ("sbuf", [128, 1024], "bfloat16"),
@@ -54,15 +54,9 @@ SCRATCH = {
     "h3": ("sbuf", [128, 4, 4, 4, 4], "bfloat16"),
     "tab": ("sbuf", [128, 4 * TS], "bfloat16"),
     "mask": ("sbuf", [128, MW], "bfloat16"),
-    "pk": ("sbuf", [128, 4 * len(PACKED) * COLS], "bfloat16"),
-    "left": ("sbuf", [128, 4 * SL], "bfloat16"),
-    "pt": ("sbuf", [128, 4 * SL], "bfloat16"),
-    "q0": ("sbuf", [128, 4 * CAPP], "float8_e4m3fn_x4"),
-    "s0": ("sbuf", [128, 4 * CAPP], "uint8"),
-    "q1": ("sbuf", [128, RUN], "float8_e4m3fn_x4"),
-    "s1": ("sbuf", [128, RUN], "uint8"),
-    "q2": ("sbuf", [128, RUN], "float8_e4m3fn_x4"),
-    "s2": ("sbuf", [128, RUN], "uint8"),
+    "pk": ("sbuf", [128, 4 * len(PACK) * 128], "bfloat16"),
+    "left": ("sbuf", [128, 4 * PW], "bfloat16"),
+    "pt": ("sbuf", [128, 4 * PW], "bfloat16"),
     "lc": ("sbuf", [128, LAND], "float8_e4m3fn_x4"),
     "ls": ("sbuf", [128, LAND], "uint8"),
     "lp": ("sbuf", [128, 32], "int32"),
@@ -73,8 +67,11 @@ SCRATCH = {
     "yt": ("sbuf", [128, P], "float32"),
     "ps": ("psum", [128, 4096], "float32"),
 }
-SEMAPHORES = ["vs", "ss", "ts", "gs", "lst", "lx", "la0", "la1", "la2", "la3", "luv", "lpl", "got0", "got1", "got2", "sent",
-              "st0", "st1"]
+for _j in range(5):
+    SCRATCH["q%d" % _j] = ("sbuf", [128, RUN], "float8_e4m3fn_x4")
+    SCRATCH["s%d" % _j] = ("sbuf", [128, RUN], "uint8")
+SEMAPHORES = ["vs", "ss", "ts", "gs", "lst", "lx", "la0", "la1", "la2", "la3", "luv", "lpl", "got0", "got1", "got2", "got3",
+              "sent", "st0", "st1"]
 
 
 def half(h, k, bit):
@@ -88,8 +85,8 @@ def falling(buf, a, w):
 
 
 def groups(rank):
-    h, p = rank // 4, rank // 2
-    return 4 * (1 - h), 2 * (p ^ 1), 2 * p
+    p = rank // 2
+    return (2 * (p ^ 2), 2), (2 * (p ^ 3), 2), (2 * (p ^ 1), 2), (rank ^ 1, 1), (rank, 1)
 
 
 def rank_program(g, core, T, topo):
@@ -100,6 +97,7 @@ def rank_program(g, core, T, topo):
     A, F = AluOpType, ActivationFunctionType
     vs, ss, ts, gs = T.sem.vs, T.sem.ss, T.sem.ts, T.sem.gs
     group = groups(rank)
+    NG = len(group) - 1
     n = {"v": 0, "s": 0, "t": 0, "g": 0}
 
     def v(i):
@@ -125,6 +123,13 @@ def rank_program(g, core, T, topo):
     def bank(b, w):
         return T.ps[:, 512 * b:512 * b + w]
 
+    span, land, at = [], [0], RUN - CAPP * group[0][1]
+    for r0, nr in group:
+        o = CAPP * r0 // 16
+        span.append((at, CAPP * nr + 16 * (o % 2), o - o % 2))
+        at += span[-1][1]
+        land.append(land[-1] + CAPP * nr)
+
     S.dma_start(T.lol[:, 0:LW], T.lo[:]).then_inc(T.sem.lst, 16)
     S.dma_start(T.lol[:, LW:2 * LW], T.ln[:]).then_inc(T.sem.lst, 16)
     Y.dma_start(T.xt[:], T.x[:]).then_inc(T.sem.lx, 16)
@@ -136,32 +141,47 @@ def rank_program(g, core, T, topo):
         Y.dma_start(T.lp[16 * k:16 * k + 16, 0:16], T.pf[:]).then_inc(T.sem.lpl, 16)
         Y.dma_start(T.lp[16 * k:16 * k + 16, 16:32], T.pg[:]).then_inc(T.sem.lpl, 16)
 
+    def cand(k, side):
+        a = PL * LW * (1 - side)
+        return T.cand[:, a + TOP - k:a + PL * LW:PL]
+
+    def floors(j, part):
+        a, b = (0, 2) if part is None else (part, part + 1)
+        return T.tj[:, PL * LW * a + TOP + 1 - j:PL * LW * b:PL]
+
     ones = v(V.memset(T.mask[:], 1.0))
-    v(V.memset(T.tj[:, 0::8], 0.0))
-    v(V.memset(T.cb[:, 7::8], 0.0))
-    v(V.memset(T.cf[:, 7::8], 0.0))
+    v(V.memset(T.pt[:, 0:4 * span[0][0]], 0.0))
+    v(V.memset(T.tj[:, 0::PL], 0.0))
     v(V.memset(T.tab[:, 0::TS], 0.0))
     v(V.memset(T.tab[:, 1 + COLS::TS], 0.0))
-    for k in range(1, LEV + 1):
-        if k not in PACKED:
-            v(V.memset(T.cb[:, 7 - k::8], BK[k] - 1.0))
-            v(V.memset(T.cf[:, 7 - k::8], FK[k] - (1 << k) - 1.0))
+    v(V.memset(T.zv[:, 0:1], 0.0))
+    v(V.memset(T.zu[:, 0:1], 0.0))
+    for k in range(LOW, TOP + 1):
+        for side in (0, 1):
+            if (k, side) not in PACK:
+                v(V.memset(cand(k, side), TB[k, side] - 1.0 - side * (COLS - width(k, side))))
 
     V.wait_ge(T.sem.lst, 32)
     v(V.tensor_scalar(T.lr[:, 0:LW], T.lol[:, 0:LW], 1, None, A.add))
     lists = v(V.tensor_tensor(T.lr[:, LW:2 * LW], T.lol[:, 0:LW], T.lol[:, LW:2 * LW], A.add))
+    v(V.tensor_scalar(T.lr[:, 2 * LW:3 * LW], T.lol[:, 0:LW], 1, None, A.add))
     V.wait_ge(vs, ones)
-    for k in range(1, LEV + 1):
-        consts = v(V.memset(T.mask[:, MK[k]:MK[k] + width(k):1 << k], 0.0))
+    for k in range(LOW, TOP + 1):
+        consts = v(V.memset(T.mask[:, MK[k]:MK[k] + max(width(k, 0), width(k, 1)):1 << k], 0.0))
+
+    def floor(out, in_, j, shift):
+        return s(S.activation(out, in_, F.Identity, bias=128.5 + (shift - 0.5) * 2.0 ** -j, scale=2.0 ** -j))
 
     S.wait_ge(vs, lists)
-    for j in range(LEV, 0, -1):
-        floors = s(S.activation(T.tj[:, 8 - j::8], T.lr[:], F.Identity, bias=128.5 - 2.0 ** -(j + 1), scale=2.0 ** -j))
-    S.wait_ge(ss, floors)
-    for j in PACKED:
-        w = 2.0 ** (j - 1)
-        s(S.activation(T.cb[:, 7 - j::8], T.tj[:, 8 * LW + 8 - j::8], F.Identity, bias=BK[j] - 1 + w + 129 * w, scale=-w))
-        cands = s(S.activation(T.cf[:, 7 - j::8], T.tj[:, 8 * LW + 8 - j::8], F.Identity, bias=FK[j] - 1 - w + 129 * w, scale=-w))
+    for j in range(TOP, LOW, -1):
+        floored = floor(floors(j, None), T.lr[:, 0:2 * LW], j, 0)
+    S.wait_ge(ss, floored)
+    for k, side in PACK:
+        w = 2.0 ** (k - 1)
+        cands = s(S.activation(cand(k, side), floors(k, 1), F.Identity, bias=TB[k, side] - 1 + (130 - 2 * side) * w, scale=-w))
+    floor(T.edge[:, 0:LW], T.lr[:, 0:LW], LOW, -1)
+    floor(T.edge[:, LW:3 * LW], T.lr[:, 0:2 * LW], LOW, 0)
+    edges = floor(T.edge[:, 3 * LW:4 * LW], T.lr[:, LW:2 * LW], LOW, 1)
 
     def product_a(i):
         V.wait_ge(T.sem["la%d" % i], 16)
@@ -170,8 +190,8 @@ def rank_program(g, core, T, topo):
         PE.wait_ge(vs, q)
         return t(PE.matmul_mx(bank(i, COLS), T.qa[:, c], T.sa[:, c], T.qx[:], T.sx[:], True, True))
 
-    def packed(i, k, bit):
-        return COLS * (len(PACKED) * i + PACKED.index(k)) + 128 * bit
+    def packed(i, key):
+        return 128 * (len(PACK) * i + list(PACK).index(key))
 
     def result(i, z):
         S.wait_ge(ts, z)
@@ -183,50 +203,51 @@ def rank_program(g, core, T, topo):
         S.wait_ge(ss, r[1])
         g.wait_ge(ss, r[1])
         ready = {}
-        for k in PACKED:
-            for bit in (0, 1):
-                a = packed(i, k, bit)
-                if k in BY_S:
-                    ready[k] = (ss, s(S.activation(T.pk[:, a:a + 128], half(h, k, bit), F.Copy)))
-                else:
-                    ready[k] = (gs, gp(g.affine_select(T.pk[:, a:a + 128], half(h, k, bit), [[0, 128]], A.is_equal, 0.0, 0, 0)))
+        for key, who in PACK.items():
+            a = packed(i, key)
+            if who == "s":
+                ready[key] = (ss, s(S.activation(T.pk[:, a:a + 128], half(h, *key), F.Copy)))
+            else:
+                ready[key] = (gs, gp(g.affine_select(T.pk[:, a:a + 128], half(h, *key), [[0, 128]], A.is_equal, 0.0, 0, 0)))
         return ready
 
-    def scans(i, k, fall, rise):
-        w = width(k)
+    def scan(i, k, side, buf, a):
+        w, to = width(k, side), TS * i + TB[k, side]
         m = T.mask[:, MK[k]:MK[k] + w]
-        v(V.tensor_tensor_scan(falling(T.tab, TS * i + BK[k], w), m, fall, 0.0, A.mult, A.max))
-        return v(V.tensor_tensor_scan(T.tab[:, TS * i + FK[k]:TS * i + FK[k] + w], m, rise, 0.0, A.mult, A.max))
+        if side:
+            return v(V.tensor_tensor_scan(T.tab[:, to:to + w], m, buf[:, a:a + w], 0.0, A.mult, A.max))
+        return v(V.tensor_tensor_scan(falling(T.tab, to, w), m, falling(buf, a, w), 0.0, A.mult, A.max))
 
     def high(i, r):
         V.wait_ge(ss, r[0])
         V.wait_ge(vs, consts)
-        for k in range(LEV, 0, -1):
-            if k not in PACKED:
-                w, h0 = width(k), TS * i + 1
-                scans(i, k, falling(T.tab, h0, w), T.tab[:, h0 + COLS - w:h0 + COLS])
+        for k in range(TOP, LOW - 1, -1):
+            for side in (0, 1):
+                if (k, side) not in PACK:
+                    scan(i, k, side, T.tab, TS * i + 1 + side * (COLS - width(k, side)))
 
     def low(i, ready):
-        for k in PACKED:
-            V.wait_ge(*ready[k])
-            a, b = packed(i, k, 0), packed(i, k, 1)
-            last = scans(i, k, falling(T.pk, a, 128), T.pk[:, b:b + 128])
+        for key in PACK:
+            V.wait_ge(*ready[key])
+            last = scan(i, key[0], key[1], T.pk, packed(i, key))
         return last
 
     V.wait_ge(T.sem.lx, 16)
     v(V.quantize_mx(T.qx[:], T.sx[:], T.xt[:]))
-    V.wait_ge(ss, floors)
-    d = v(V.tensor_tensor(T.dif[:], T.tj[:, 8 * LW:16 * LW], T.tj[:, 0:8 * LW], A.is_gt))
+    V.wait_ge(ss, floored)
+    d = v(V.tensor_tensor(T.dif[:], T.tj[:, PL * LW:2 * PL * LW], T.tj[:, 0:PL * LW], A.is_gt))
     z0 = product_a(0)
     V.wait_ge(ss, cands)
     V.wait_ge(vs, d)
-    b = v(V.tensor_tensor_scan(T.pb[:], T.dif[:], T.cb[:], 0.0, A.mult, A.max))
-    f = v(V.tensor_tensor_scan(T.pq[:], T.dif[:], T.cf[:], 0.0, A.mult, A.max))
-    V.wait_ge(vs, b)
-    v(V.tensor_tensor(T.offl[:], T.pb[:, 7::8], T.lr[:, 0:LW], A.add))
-    V.wait_ge(vs, f)
-    offs = v(V.tensor_tensor(T.offr[:], T.pq[:, 7::8], T.lr[:, LW:2 * LW], A.add))
+    for a in (0, PL * LW):
+        picked = v(V.tensor_tensor_scan(T.pick[:, a:a + PL * LW], T.dif[:], T.cand[:, a:a + PL * LW], 0.0, A.mult, A.max))
+    V.wait_ge(ss, edges)
+    d = v(V.tensor_tensor(T.dlow[:], T.edge[:, 2 * LW:4 * LW], T.edge[:, 0:2 * LW], A.is_gt))
     z1 = product_a(1)
+    V.wait_ge(vs, d)
+    b = v(V.tensor_tensor(T.base[:], T.pick[:, PL - 1::PL], T.dlow[:], A.mult))
+    V.wait_ge(vs, b)
+    offs = v(V.tensor_tensor(T.off[:], T.base[:], T.lr[:, LW:3 * LW], A.add))
     r0 = result(0, z0)
     r1 = result(1, z1)
     p0 = pack(0, r0)
@@ -245,81 +266,82 @@ def rank_program(g, core, T, topo):
     w3 = low(3, p3)
 
     def left(j):
-        k, w, o = AT[j], AT[j + 1] - AT[j], CAPP * group[j] // 16
+        k, w, o = span[j]
         done = []
         for i, c in enumerate((w0, w1, w2, w3)):
             S.wait_ge(vs, max(c, offs))
-            done.append(s(S.activation(T.left[:, SL * i + k:SL * i + k + w],
-                                       T.tab[:, TS * i:TS * i + TW].indirect(T.offl[:, o:o + w // 16]), F.Copy)))
+            done.append(s(S.activation(T.left[:, PW * i + k:PW * i + k + w],
+                                       T.tab[:, TS * i:TS * i + TW].indirect(T.off[:, LW + o:LW + o + w // 16]), F.Copy)))
         return done
 
     def right(j, lefts):
-        k, w, o = AT[j], AT[j + 1] - AT[j], CAPP * group[j] // 16
+        k, w, o = span[j]
         V.wait_ge(vs, offs)
         for i in range(4):
             V.wait_ge(ss, lefts[i])
             full = v(V.tensor_tensor(T.pt[:, 4 * k + i:4 * (k + w):4],
-                                     T.tab[:, TS * i:TS * i + TW].indirect(T.offr[:, o:o + w // 16]),
-                                     T.left[:, SL * i + k:SL * i + k + w], A.max))
+                                     T.tab[:, TS * i:TS * i + TW].indirect(T.off[:, o:o + w // 16]),
+                                     T.left[:, PW * i + k:PW * i + k + w], A.max))
         V.wait_ge(vs, full)
-        w = max(w, RUN)
-        return v(V.quantize_mx(T["q%d" % j][:], T["s%d" % j][:], T.pt[:, 4 * (AT[j + 1] - w):4 * AT[j + 1]]))
+        return v(V.quantize_mx(T["q%d" % j][:], T["s%d" % j][:], T.pt[:, 4 * (k + w - RUN):4 * (k + w)]))
 
     def send(j, q):
-        to = [r for r in range(group[j], group[j] + (AT[j + 1] - AT[j]) // CAPP) if r != rank]
-        first = RUN - 2 * CAPP if j else 0
+        r0, nr = group[j]
         g.wait_ge(vs, q)
         for src, dst, codes in (("q%d" % j, "lc", True), ("s%d" % j, "ls", False)):
             tr = []
-            for i, r in enumerate(to):
-                d = T.cores[r]
+            for i in range(nr):
+                d = T.cores[r0 + i]
                 rid, pid = topo.addr(d, core)
-                at = AT[j] + CAPP * (rank - groups(r)[j] if j < 2 else 0)
-                c = first + CAPP * (r - group[j])
-                a, b = T[src][:, c:c + CAPP], T[dst][:, at:at + CAPP]
+                to = land[j] + CAPP * (rank - groups(r0 + i)[j][0])
+                c = RUN - CAPP * (nr - i)
+                a, b = T[src][:, c:c + CAPP], T[dst][:, to:to + CAPP]
                 if codes:
                     a, b = a.bitcast(dt.uint8), b.bitcast(dt.uint8)
                 e = topo.engines(core, d)
-                w = len(e) // len(to)
+                w = len(e) // nr
                 tr.append(RemoteDMATransfer(dst_ids=[DstId(rid=rid, pnc=pid)], dma_engine_mask=sum(1 << x for x in e[w * i:w * i + w]),
                                             remote_sem=T.sem["got%d" % j], src=a, dst=b))
             g.remote_dma_fused(tr, local_sem=T.sem.sent)
-        return 2 * w * len(to)
+        return 2 * w * nr
 
-    lefts = [left(j) for j in range(3)]
+    lefts = [left(j) for j in range(NG + 1)]
     sent = 0
-    for j in range(3):
-        last = right(j, lefts[j])
-        sent = sent + send(j, last)
+    for j in range(NG):
+        sent = sent + send(j, right(j, lefts[j]))
 
     V.wait_ge(T.sem.luv, 32)
     quv = v(V.quantize_mx(T.quv[:], T.suv[:], T.uvt[:]))
-    v(V.memset(T.zv[:, 0:1], 0.0))
-    v(V.memset(T.zu[:, 0:1], 0.0))
+    own = right(NG, lefts[NG])
     V.wait_ge(T.sem.lpl, 256)
     places = v(V.tensor_scalar(T.offp[:], T.lp[:], 1, None, A.add))
 
-    def products(bv, codes, scales, a, b, lo, hi, slot):
-        for bk, c0 in ((bv, 128), (bv + 1, 0)):
+    def products(bv, codes, scales, a, b, parts, last=False):
+        cu = None
+        for bk, c0, to in ((bv, 128, T.zv), (bv + 1, 0, T.zu)):
             z = t(PE.matmul_mx(bank(bk, b - a), T.quv[:, c0:c0 + 128], T.suv[:, c0:c0 + 128], codes[:, a:b], scales[:, a:b], True, True))
-            src = T.ps[:, 512 * bk + lo - a:512 * bk + hi - a]
-            if c0:
-                S.wait_ge(ts, z)
-                cv = s(S.activation(T.zv[:, 1 + slot:1 + slot + hi - lo], src, F.Copy))
-            else:
-                V.wait_ge(ts, z)
-                cu = v(V.tensor_copy(T.zu[:, 1 + slot:1 + slot + hi - lo], src))
+            for lo, j in parts:
+                slot, w = CAPP * group[j][0], CAPP * group[j][1]
+                src = T.ps[:, 512 * bk + lo - a:512 * bk + lo - a + w]
+                if c0 or not last:
+                    S.wait_ge(ts, z)
+                    cv = s(S.activation(to[:, 1 + slot:1 + slot + w], src, F.Copy))
+                else:
+                    V.wait_ge(ts, z)
+                    cu = v(V.tensor_copy(to[:, 1 + slot:1 + slot + w], src))
         return cv, cu
 
-    own = RUN - 2 * CAPP + CAPP * (rank - group[2])
     PE.wait_ge(vs, quv)
-    PE.wait_ge(ss, lefts[2][3])
-    products(4, T.q2, T.s2, 0, RUN, own, own + CAPP, CAPP * rank)
-    for j, bk in ((0, 6), (1, 0), (2, 2)):
-        end = AT[j + 1] if j < 2 else LAND
-        PE.wait_ge(T.sem["got%d" % j], 16)
-        slot = CAPP * (group[j] if j < 2 else rank ^ 1)
-        cv, cu = products(bk, T.lc, T.ls, end - max(end - AT[j], RUN), end, AT[j], end, slot)
+    PE.wait_ge(ss, lefts[NG][3])
+    PE.wait_ge(T.sem.got0, 16)
+    PE.wait_ge(T.sem.got1, 16)
+    products(6, T.lc, T.ls, 0, land[2], [(land[0], 0), (land[1], 1)])
+    PE.wait_ge(vs, own)
+    products(4, T["q%d" % NG], T["s%d" % NG], 0, RUN, [(RUN - CAPP, NG)])
+    PE.wait_ge(T.sem.got2, 16)
+    products(0, T.lc, T.ls, land[3] - RUN, land[3], [(land[2], 2)])
+    PE.wait_ge(T.sem.got3, 16)
+    cv, cu = products(2, T.lc, T.ls, LAND - RUN, LAND, [(land[3], 3)], True)
 
     S.wait_ge(vs, places)
     S.wait_ge(ss, cv)

@@ -6,7 +6,7 @@ SL = N * CAPP
 LW = SL // 16
 LAND = (N - 1) * CAPP
 RUN = 128
-PW = 448
+PW = 480
 LOW, TOP = 2, 7
 PL = TOP - LOW + 1
 PACK = {(4, 0): "s", (4, 1): "s", (5, 0): "s", (3, 0): "g", (3, 1): "g"}
@@ -18,7 +18,7 @@ def width(k, side):
 
 
 def layout():
-    tb, m, at, am = {}, {}, 2 + COLS, 0
+    tb, m, at, am = {}, {}, 1 + COLS, 0
     for k in range(LOW, TOP + 1):
         tb[k, 0], tb[k, 1], m[k] = at, at + width(k, 0), am
         at, am = at + width(k, 0) + width(k, 1), am + max(width(k, 0), width(k, 1))
@@ -30,6 +30,7 @@ TS = (TW + 15) // 16 * 16
 
 SCRATCH = {
     "lol": ("sbuf", [128, 2 * LW], "int32"),
+    "one": ("sbuf", [128, 2 * LW], "float32"),
     "lr": ("sbuf", [128, 3 * LW], "float32"),
     "tj": ("sbuf", [128, 2 * PL * LW], "bfloat16"),
     "edge": ("sbuf", [128, 4 * LW], "bfloat16"),
@@ -70,7 +71,7 @@ SCRATCH = {
 for _j in range(5):
     SCRATCH["q%d" % _j] = ("sbuf", [128, RUN], "float8_e4m3fn_x4")
     SCRATCH["s%d" % _j] = ("sbuf", [128, RUN], "uint8")
-SEMAPHORES = ["vs", "ss", "ts", "gs", "lst", "lx", "la0", "la1", "la2", "la3", "luv", "lpl", "got0", "got1", "got2", "got3",
+SEMAPHORES = ["vs", "ss", "ts", "gs", "lst", "lx0", "lx1", "la0", "la1", "la2", "la3", "luv", "lpl", "got0", "got1", "got2", "got3",
               "sent", "st0", "st1"]
 
 
@@ -86,7 +87,7 @@ def falling(buf, a, w):
 
 def groups(rank):
     p = rank // 2
-    return (2 * (p ^ 2), 2), (2 * (p ^ 3), 2), (2 * (p ^ 1), 2), (rank ^ 1, 1), (rank, 1)
+    return (rank ^ 1, 1), (2 * (p ^ 2), 2), (2 * (p ^ 3), 2), (2 * (p ^ 1), 2), (rank, 1)
 
 
 def rank_program(g, core, T, topo):
@@ -123,7 +124,7 @@ def rank_program(g, core, T, topo):
     def bank(b, w):
         return T.ps[:, 512 * b:512 * b + w]
 
-    span, land, at = [], [0], RUN - CAPP * group[0][1]
+    span, land, at = [], [0], RUN - CAPP * group[0][1] - 16 * (group[0][0] % 2)
     for r0, nr in group:
         o = CAPP * r0 // 16
         span.append((at, CAPP * nr + 16 * (o % 2), o - o % 2))
@@ -131,10 +132,11 @@ def rank_program(g, core, T, topo):
         land.append(land[-1] + CAPP * nr)
 
     S.dma_start(T.lol[:, 0:LW], T.lo[:]).then_inc(T.sem.lst, 16)
-    S.dma_start(T.lol[:, LW:2 * LW], T.ln[:]).then_inc(T.sem.lst, 16)
-    Y.dma_start(T.xt[:], T.x[:]).then_inc(T.sem.lx, 16)
+    Y.dma_start(T.lol[:, LW:2 * LW], T.ln[:]).then_inc(T.sem.lst, 16)
     for i in range(4):
-        Y.dma_start(T["at"][:, 512 * i:512 * i + 512], T.a[:, 512 * i:512 * i + 512]).then_inc(T.sem["la%d" % i], 16)
+        if i < 2:
+            Y.dma_start(T.xt[:, 512 * i:512 * i + 512], T.x[:, 512 * i:512 * i + 512]).then_inc(T.sem["lx%d" % i], 16)
+        (Y if i else S).dma_start(T["at"][:, 512 * i:512 * i + 512], T.a[:, 512 * i:512 * i + 512]).then_inc(T.sem["la%d" % i], 16)
     Y.dma_start(T.uvt[:, 0:512], T.u[:]).then_inc(T.sem.luv, 16)
     Y.dma_start(T.uvt[:, 512:1024], T.v[:]).then_inc(T.sem.luv, 16)
     for k in range(8):
@@ -149,39 +151,44 @@ def rank_program(g, core, T, topo):
         a, b = (0, 2) if part is None else (part, part + 1)
         return T.tj[:, PL * LW * a + TOP + 1 - j:PL * LW * b:PL]
 
-    ones = v(V.memset(T.mask[:], 1.0))
-    v(V.memset(T.pt[:, 0:4 * span[0][0]], 0.0))
-    v(V.memset(T.tj[:, 0::PL], 0.0))
-    v(V.memset(T.tab[:, 0::TS], 0.0))
-    v(V.memset(T.tab[:, 1 + COLS::TS], 0.0))
-    v(V.memset(T.zv[:, 0:1], 0.0))
-    v(V.memset(T.zu[:, 0:1], 0.0))
+    S.wait_ge(vs, v(V.memset(T.one[:], 1.0)))
+    g.wait_ge(vs, v(V.memset(T.mask[:], 1.0)))
+
+    def fill(ap, w, c):
+        return s(S.activation(ap, T.one[:, 0:w], F.Identity, scale=float(c)))
+
+    fill(T.tj[:, 0::PL], 2 * LW, 0)
     for k in range(LOW, TOP + 1):
         for side in (0, 1):
             if (k, side) not in PACK:
-                v(V.memset(cand(k, side), TB[k, side] - 1.0 - side * (COLS - width(k, side))))
+                fill(cand(k, side), LW, TB[k, side] - 1 - side * (COLS - width(k, side)))
+    fill(T.tab[:, 0::TS], 4, 0)
+    fill(T.zv[:, 0:1], 1, 0)
+    fill(T.zu[:, 0:1], 1, 0)
+    for k in range(TOP, LOW - 1, -1):
+        w = max(width(k, 0), width(k, 1))
+        gp(g.iota(T.mask[:, MK[k]:MK[k] + w:1 << k], [[0, w >> k]], 0, 0, allow_small_or_imprecise_dtypes=True))
+    consts = gp(g.iota(T.pt[:, 0:4 * span[0][0]], [[0, 4 * span[0][0]]], 0, 0, allow_small_or_imprecise_dtypes=True))
 
     V.wait_ge(T.sem.lst, 32)
     v(V.tensor_scalar(T.lr[:, 0:LW], T.lol[:, 0:LW], 1, None, A.add))
     lists = v(V.tensor_tensor(T.lr[:, LW:2 * LW], T.lol[:, 0:LW], T.lol[:, LW:2 * LW], A.add))
     v(V.tensor_scalar(T.lr[:, 2 * LW:3 * LW], T.lol[:, 0:LW], 1, None, A.add))
-    V.wait_ge(vs, ones)
-    for k in range(LOW, TOP + 1):
-        consts = v(V.memset(T.mask[:, MK[k]:MK[k] + max(width(k, 0), width(k, 1)):1 << k], 0.0))
 
-    def floor(out, in_, j, shift):
-        return s(S.activation(out, in_, F.Identity, bias=128.5 + (shift - 0.5) * 2.0 ** -j, scale=2.0 ** -j))
+    def bias(j, shift):
+        return 128.5 + (shift - 0.5) * 2.0 ** -j
 
     S.wait_ge(vs, lists)
-    for j in range(TOP, LOW, -1):
-        floored = floor(floors(j, None), T.lr[:, 0:2 * LW], j, 0)
-    S.wait_ge(ss, floored)
+    for j in range(LOW + 1, TOP + 1):
+        floored = s(S.activation(floors(j, None), T.lr[:, 0:2 * LW], F.Identity, bias=bias(j, 0), scale=2.0 ** -j))
+    V.wait_ge(vs, lists)
+    for a, b, c, shift in ((0, 1, 0, -1), (1, 3, 0, 0), (3, 4, 1, 1)):
+        edges = v(V.tensor_scalar(T.edge[:, LW * a:LW * b], T.lr[:, LW * c:LW * (c + b - a)], 2.0 ** -LOW, bias(LOW, shift),
+                                  A.mult, A.add))
+    S.wait_ge(ss, floored - (TOP - max(k for k, side in PACK)))
     for k, side in PACK:
         w = 2.0 ** (k - 1)
         cands = s(S.activation(cand(k, side), floors(k, 1), F.Identity, bias=TB[k, side] - 1 + (130 - 2 * side) * w, scale=-w))
-    floor(T.edge[:, 0:LW], T.lr[:, 0:LW], LOW, -1)
-    floor(T.edge[:, LW:3 * LW], T.lr[:, 0:2 * LW], LOW, 0)
-    edges = floor(T.edge[:, 3 * LW:4 * LW], T.lr[:, LW:2 * LW], LOW, 1)
 
     def product_a(i):
         V.wait_ge(T.sem["la%d" % i], 16)
@@ -195,8 +202,8 @@ def rank_program(g, core, T, topo):
 
     def result(i, z):
         S.wait_ge(ts, z)
-        r = s(S.activation(T.tab[:, TS * i + 1:TS * i + 1 + COLS], bank(i, COLS), F.Relu, scale=0.05))
-        return r, s(S.activation(T["h%d" % i][:], bank(i, COLS), F.Relu, scale=0.05))
+        r = s(S.activation(T["h%d" % i][:], bank(i, COLS), F.Relu, scale=0.05))
+        return s(S.activation(T.tab[:, TS * i + 1:TS * i + 1 + COLS], bank(i, COLS), F.Relu, scale=0.05)), r
 
     def pack(i, r):
         h = T["h%d" % i]
@@ -220,7 +227,7 @@ def rank_program(g, core, T, topo):
 
     def high(i, r):
         V.wait_ge(ss, r[0])
-        V.wait_ge(vs, consts)
+        V.wait_ge(gs, consts)
         for k in range(TOP, LOW - 1, -1):
             for side in (0, 1):
                 if (k, side) not in PACK:
@@ -232,27 +239,42 @@ def rank_program(g, core, T, topo):
             last = scan(i, key[0], key[1], T.pk, packed(i, key))
         return last
 
-    V.wait_ge(T.sem.lx, 16)
-    v(V.quantize_mx(T.qx[:], T.sx[:], T.xt[:]))
+    def half_x(k):
+        V.wait_ge(T.sem["lx%d" % k], 16)
+        return v(V.quantize_mx(T.qx[:, 128 * k:128 * k + 128], T.sx[:, 128 * k:128 * k + 128], T.xt[:, 512 * k:512 * k + 512]))
+
+    def half_z(k, q):
+        c = slice(128 * k, 128 * k + 128)
+        PE.wait_ge(vs, q)
+        return t(PE.matmul_mx(bank(4 * k, 128), T.qa[:, 0:128], T.sa[:, 0:128], T.qx[:, c], T.sx[:, c], True, True))
+
+    half_x(0)
+    V.wait_ge(T.sem.la0, 16)
+    z0 = [half_z(0, v(V.quantize_mx(T.qa[:, 0:128], T.sa[:, 0:128], T["at"][:, 0:512])))]
     V.wait_ge(ss, floored)
-    d = v(V.tensor_tensor(T.dif[:], T.tj[:, PL * LW:2 * PL * LW], T.tj[:, 0:PL * LW], A.is_gt))
-    z0 = product_a(0)
-    V.wait_ge(ss, cands)
+    v(V.tensor_tensor(T.dif[:], T.tj[:, PL * LW:2 * PL * LW], T.tj[:, 0:PL * LW], A.is_gt))
+    V.wait_ge(vs, edges)
+    d = v(V.tensor_tensor(T.dlow[:], T.edge[:, 2 * LW:4 * LW], T.edge[:, 0:2 * LW], A.is_gt))
+    z0.append(half_z(1, half_x(1)))
     V.wait_ge(vs, d)
+    V.wait_ge(ss, cands)
     for a in (0, PL * LW):
         picked = v(V.tensor_tensor_scan(T.pick[:, a:a + PL * LW], T.dif[:], T.cand[:, a:a + PL * LW], 0.0, A.mult, A.max))
-    V.wait_ge(ss, edges)
-    d = v(V.tensor_tensor(T.dlow[:], T.edge[:, 2 * LW:4 * LW], T.edge[:, 0:2 * LW], A.is_gt))
     z1 = product_a(1)
-    V.wait_ge(vs, d)
+    V.wait_ge(vs, picked)
     b = v(V.tensor_tensor(T.base[:], T.pick[:, PL - 1::PL], T.dlow[:], A.mult))
-    V.wait_ge(vs, b)
-    offs = v(V.tensor_tensor(T.off[:], T.base[:], T.lr[:, LW:3 * LW], A.add))
-    r0 = result(0, z0)
+    S.wait_ge(ts, z0[0])
+    s(S.activation(T.tab[:, 1:129], bank(0, 128), F.Relu, scale=0.05))
+    s(S.activation(T.h0[:, 0:2], bank(0, 128), F.Relu, scale=0.05))
+    S.wait_ge(ts, z0[1])
+    r0 = (s(S.activation(T.tab[:, 129:257], bank(4, 128), F.Relu, scale=0.05)),
+          s(S.activation(T.h0[:, 2:4], bank(4, 128), F.Relu, scale=0.05)))
     r1 = result(1, z1)
     p0 = pack(0, r0)
     p1 = pack(1, r1)
     high(0, r0)
+    V.wait_ge(vs, b)
+    offs = v(V.tensor_tensor(T.off[:], T.base[:], T.lr[:, LW:3 * LW], A.add))
     r2 = result(2, product_a(2))
     p2 = pack(2, r2)
     high(1, r1)
@@ -274,14 +296,17 @@ def rank_program(g, core, T, topo):
                                        T.tab[:, TS * i:TS * i + TW].indirect(T.off[:, LW + o:LW + o + w // 16]), F.Copy)))
         return done
 
-    def right(j, lefts):
+    def right(j, results):
         k, w, o = span[j]
-        V.wait_ge(vs, offs)
-        for i in range(4):
-            V.wait_ge(ss, lefts[i])
+        for i in results:
+            V.wait_ge(ss, lefts[j][i])
             full = v(V.tensor_tensor(T.pt[:, 4 * k + i:4 * (k + w):4],
                                      T.tab[:, TS * i:TS * i + TW].indirect(T.off[:, o:o + w // 16]),
                                      T.left[:, PW * i + k:PW * i + k + w], A.max))
+        return full
+
+    def quantise(j, full):
+        k, w, o = span[j]
         V.wait_ge(vs, full)
         return v(V.quantize_mx(T["q%d" % j][:], T["s%d" % j][:], T.pt[:, 4 * (k + w - RUN):4 * (k + w)]))
 
@@ -299,6 +324,8 @@ def rank_program(g, core, T, topo):
                 if codes:
                     a, b = a.bitcast(dt.uint8), b.bitcast(dt.uint8)
                 e = topo.engines(core, d)
+                if j == 0:
+                    e = e[0::2] if codes else e[1::2]
                 w = len(e) // nr
                 tr.append(RemoteDMATransfer(dst_ids=[DstId(rid=rid, pnc=pid)], dma_engine_mask=sum(1 << x for x in e[w * i:w * i + w]),
                                             remote_sem=T.sem["got%d" % j], src=a, dst=b))
@@ -307,14 +334,19 @@ def rank_program(g, core, T, topo):
 
     lefts = [left(j) for j in range(NG + 1)]
     sent = 0
-    for j in range(NG):
-        sent = sent + send(j, right(j, lefts[j]))
+    sent = send(0, quantise(0, right(0, [0, 1, 2, 3])))
+    right(1, [0])
+    for j in range(1, NG):
+        full = right(j, [1, 2, 3])
+        right(j + 1, [0])
+        sent = sent + send(j, quantise(j, full))
 
     V.wait_ge(T.sem.luv, 32)
     quv = v(V.quantize_mx(T.quv[:], T.suv[:], T.uvt[:]))
-    own = right(NG, lefts[NG])
+    full = right(NG, [1, 2, 3])
     V.wait_ge(T.sem.lpl, 256)
     places = v(V.tensor_scalar(T.offp[:], T.lp[:], 1, None, A.add))
+    own = quantise(NG, full)
 
     def products(bv, codes, scales, a, b, parts, last=False):
         cu = None
@@ -333,13 +365,13 @@ def rank_program(g, core, T, topo):
 
     PE.wait_ge(vs, quv)
     PE.wait_ge(ss, lefts[NG][3])
-    PE.wait_ge(T.sem.got0, 16)
+    PE.wait_ge(T.sem.got0, 8)
     PE.wait_ge(T.sem.got1, 16)
     products(6, T.lc, T.ls, 0, land[2], [(land[0], 0), (land[1], 1)])
     PE.wait_ge(vs, own)
-    products(4, T["q%d" % NG], T["s%d" % NG], 0, RUN, [(RUN - CAPP, NG)])
+    products(4, T["q%d" % NG], T["s%d" % NG], 0, RUN, [(RUN - CAPP, NG)], True)
     PE.wait_ge(T.sem.got2, 16)
-    products(0, T.lc, T.ls, land[3] - RUN, land[3], [(land[2], 2)])
+    products(0, T.lc, T.ls, land[3] - RUN, land[3], [(land[2], 2)], True)
     PE.wait_ge(T.sem.got3, 16)
     cv, cu = products(2, T.lc, T.ls, LAND - RUN, LAND, [(land[3], 3)], True)
 

@@ -9,7 +9,9 @@ RUN = 128
 PW = 480
 LOW, TOP = 2, 7
 PL = TOP - LOW + 1
-PACK = {(4, 0): "s", (4, 1): "s", (5, 0): "s", (3, 0): "g", (3, 1): "g"}
+PACK = {(3, 0): "gggg", (3, 1): "gggg", (4, 0): "ssss", (5, 0): "ssss", (4, 1): "ssss", (5, 1): "ssss"}
+ORDER = "o0 x1 o1 z1 o2 e0 e1 f0 f1 h1 c1 u0 z2 o3 p0 h2 c2 u1 z3 p1 h3 c3 l0 u2 p2 l1 u3 p3 l2 l3"
+CUT = 128
 ZW = 392
 
 
@@ -18,14 +20,20 @@ def width(k, side):
 
 
 def layout():
-    tb, m, at, am = {}, {}, 1 + COLS, 0
-    for k in range(LOW, TOP + 1):
-        tb[k, 0], tb[k, 1], m[k] = at, at + width(k, 0), am
-        at, am = at + width(k, 0) + width(k, 1), am + max(width(k, 0), width(k, 1))
+    tb, at = {}, 1 + COLS
+    for side in (0, 1):
+        for k in range(LOW, TOP + 1):
+            tb[k, side], at = at, at + width(k, side)
+    m, am = [], 0
+    for k in [LOW] + list(range(TOP, LOW, -1)) + [k for k, side in RUNS[1][1:]]:
+        m.append((k, am, max(width(k, 0), width(k, 1))))
+        am += m[-1][2]
     return tb, m, at, am
 
 
-TB, MK, TW, MW = layout()
+RUNS = [sorted(key for key in PACK if key[1] == side) for side in (0, 1)]
+TB, MASKS, TW, MW = layout()
+MK = {k: a for k, a, w in MASKS[::-1]}
 TS = (TW + 15) // 16 * 16
 
 SCRATCH = {
@@ -40,6 +48,7 @@ SCRATCH = {
     "pick": ("sbuf", [128, 2 * PL * LW], "float32"),
     "base": ("sbuf", [128, 2 * LW], "float32"),
     "off": ("sbuf", [128, 2 * LW], "uint16"),
+    "off0": ("sbuf", [128, 2 * LW], "uint16"),
     "xt": ("sbuf", [128, 1024], "bfloat16"),
     "at": ("sbuf", [128, 2048], "bfloat16"),
     "uvt": ("sbuf", [128, 1024], "bfloat16"),
@@ -55,7 +64,7 @@ SCRATCH = {
     "h3": ("sbuf", [128, 4, 4, 4, 4], "bfloat16"),
     "tab": ("sbuf", [128, 4 * TS], "bfloat16"),
     "mask": ("sbuf", [128, MW], "bfloat16"),
-    "pk": ("sbuf", [128, 4 * len(PACK) * 128], "bfloat16"),
+    "pk": ("sbuf", [128, 4, len(PACK) * 128], "bfloat16"),
     "left": ("sbuf", [128, 4 * PW], "bfloat16"),
     "pt": ("sbuf", [128, 4 * PW], "bfloat16"),
     "lc": ("sbuf", [128, LAND], "float8_e4m3fn_x4"),
@@ -71,7 +80,7 @@ SCRATCH = {
 for _j in range(5):
     SCRATCH["q%d" % _j] = ("sbuf", [128, RUN], "float8_e4m3fn_x4")
     SCRATCH["s%d" % _j] = ("sbuf", [128, RUN], "uint8")
-SEMAPHORES = ["vs", "ss", "ts", "gs", "lst", "lx0", "lx1", "la0", "la1", "la2", "la3", "luv", "lpl", "got0", "got1", "got2", "got3",
+SEMAPHORES = ["vs", "ss", "ts", "gs", "lst", "lx0", "lx1", "la0", "la1", "la2", "la3", "luv", "lpl", "lof", "got0", "got1", "got2", "got3",
               "sent", "st0", "st1"]
 
 
@@ -81,8 +90,8 @@ def half(h, k, bit):
     return h[tuple(ix)]
 
 
-def falling(buf, a, w):
-    return buf[:, a + w - 1:(a - 1 if a else None):-1]
+def falling(a, w):
+    return slice(a + w - 1, a - 1 if a else None, -1)
 
 
 def groups(rank):
@@ -124,9 +133,9 @@ def rank_program(g, core, T, topo):
     def bank(b, w):
         return T.ps[:, 512 * b:512 * b + w]
 
-    span, land, at = [], [0], RUN - CAPP * group[0][1] - 16 * (group[0][0] % 2)
+    span, land, at = [], [0], RUN - CAPP * group[0][1]
     for r0, nr in group:
-        o = CAPP * r0 // 16
+        o = CAPP * r0 // 16 if span else 0
         span.append((at, CAPP * nr + 16 * (o % 2), o - o % 2))
         at += span[-1][1]
         land.append(land[-1] + CAPP * nr)
@@ -139,9 +148,6 @@ def rank_program(g, core, T, topo):
         (Y if i else S).dma_start(T["at"][:, 512 * i:512 * i + 512], T.a[:, 512 * i:512 * i + 512]).then_inc(T.sem["la%d" % i], 16)
     Y.dma_start(T.uvt[:, 0:512], T.u[:]).then_inc(T.sem.luv, 16)
     Y.dma_start(T.uvt[:, 512:1024], T.v[:]).then_inc(T.sem.luv, 16)
-    for k in range(8):
-        Y.dma_start(T.lp[16 * k:16 * k + 16, 0:16], T.pf[:]).then_inc(T.sem.lpl, 16)
-        Y.dma_start(T.lp[16 * k:16 * k + 16, 16:32], T.pg[:]).then_inc(T.sem.lpl, 16)
 
     def cand(k, side):
         a = PL * LW * (1 - side)
@@ -165,10 +171,9 @@ def rank_program(g, core, T, topo):
     fill(T.tab[:, 0::TS], 4, 0)
     fill(T.zv[:, 0:1], 1, 0)
     fill(T.zu[:, 0:1], 1, 0)
-    for k in range(TOP, LOW - 1, -1):
-        w = max(width(k, 0), width(k, 1))
-        gp(g.iota(T.mask[:, MK[k]:MK[k] + w:1 << k], [[0, w >> k]], 0, 0, allow_small_or_imprecise_dtypes=True))
-    consts = gp(g.iota(T.pt[:, 0:4 * span[0][0]], [[0, 4 * span[0][0]]], 0, 0, allow_small_or_imprecise_dtypes=True))
+    for k, a, w in MASKS:
+        consts = gp(g.iota(T.mask[:, a:a + w:1 << k], [[0, w >> k]], 0, 0, allow_small_or_imprecise_dtypes=True))
+    gp(g.iota(T.pt[:, 0:4 * span[0][0]], [[0, 4 * span[0][0]]], 0, 0, allow_small_or_imprecise_dtypes=True))
 
     V.wait_ge(T.sem.lst, 32)
     v(V.tensor_scalar(T.lr[:, 0:LW], T.lol[:, 0:LW], 1, None, A.add))
@@ -179,14 +184,20 @@ def rank_program(g, core, T, topo):
         return 128.5 + (shift - 0.5) * 2.0 ** -j
 
     S.wait_ge(vs, lists)
-    for j in range(LOW + 1, TOP + 1):
-        floored = s(S.activation(floors(j, None), T.lr[:, 0:2 * LW], F.Identity, bias=bias(j, 0), scale=2.0 ** -j))
     V.wait_ge(vs, lists)
+    for j in range(LOW + 1, TOP + 1):
+        if j < TOP - 1:
+            floored = s(S.activation(floors(j, None), T.lr[:, 0:2 * LW], F.Identity, bias=bias(j, 0), scale=2.0 ** -j))
+        else:
+            upper = v(V.tensor_scalar(floors(j, None), T.lr[:, 0:2 * LW], 2.0 ** -j, bias(j, 0), A.mult, A.add))
     for a, b, c, shift in ((0, 1, 0, -1), (1, 3, 0, 0), (3, 4, 1, 1)):
         edges = v(V.tensor_scalar(T.edge[:, LW * a:LW * b], T.lr[:, LW * c:LW * (c + b - a)], 2.0 ** -LOW, bias(LOW, shift),
                                   A.mult, A.add))
-    S.wait_ge(ss, floored - (TOP - max(k for k, side in PACK)))
-    for k, side in PACK:
+    V.wait_ge(ss, floored)
+    V.wait_ge(vs, upper)
+    v(V.tensor_tensor(T.dif[:], T.tj[:, PL * LW:2 * PL * LW], T.tj[:, 0:PL * LW], A.is_gt))
+    S.wait_ge(ss, floored)
+    for k, side in sorted(PACK):
         w = 2.0 ** (k - 1)
         cands = s(S.activation(cand(k, side), floors(k, 1), F.Identity, bias=TB[k, side] - 1 + (130 - 2 * side) * w, scale=-w))
 
@@ -197,46 +208,43 @@ def rank_program(g, core, T, topo):
         PE.wait_ge(vs, q)
         return t(PE.matmul_mx(bank(i, COLS), T.qa[:, c], T.sa[:, c], T.qx[:], T.sx[:], True, True))
 
-    def packed(i, key):
-        return 128 * (len(PACK) * i + list(PACK).index(key))
+    def packed(key):
+        return 128 * (RUNS[0] + RUNS[1]).index(key)
 
-    def result(i, z):
+    def relu(out, i, z):
         S.wait_ge(ts, z)
-        r = s(S.activation(T["h%d" % i][:], bank(i, COLS), F.Relu, scale=0.05))
-        return s(S.activation(T.tab[:, TS * i + 1:TS * i + 1 + COLS], bank(i, COLS), F.Relu, scale=0.05)), r
+        return s(S.activation(out, bank(i, COLS), F.Relu, scale=0.05))
 
-    def pack(i, r):
-        h = T["h%d" % i]
-        S.wait_ge(ss, r[1])
-        g.wait_ge(ss, r[1])
-        ready = {}
-        for key, who in PACK.items():
-            a = packed(i, key)
-            if who == "s":
-                ready[key] = (ss, s(S.activation(T.pk[:, a:a + 128], half(h, *key), F.Copy)))
-            else:
-                ready[key] = (gs, gp(g.affine_select(T.pk[:, a:a + 128], half(h, *key), [[0, 128]], A.is_equal, 0.0, 0, 0)))
-        return ready
+    def pack(i, key, r):
+        h, to = T["h%d" % i], T.pk[:, i, packed(key):packed(key) + 128]
+        if PACK[key][i] == "s":
+            S.wait_ge(ss, r)
+            return ss, s(S.activation(to, half(h, *key), F.Copy))
+        g.wait_ge(ss, r)
+        return gs, gp(g.affine_select(to, half(h, *key), [[0, 128]], A.is_equal, 0.0, 0, 0))
 
-    def scan(i, k, side, buf, a):
-        w, to = width(k, side), TS * i + TB[k, side]
-        m = T.mask[:, MK[k]:MK[k] + w]
+    def scan(i, k, side, buf, a, w, m):
+        to, m = TS * i + TB[k, side], T.mask[:, m:m + w]
         if side:
-            return v(V.tensor_tensor_scan(T.tab[:, to:to + w], m, buf[:, a:a + w], 0.0, A.mult, A.max))
-        return v(V.tensor_tensor_scan(falling(T.tab, to, w), m, falling(buf, a, w), 0.0, A.mult, A.max))
+            return v(V.tensor_tensor_scan(T.tab[:, to:to + w], m, buf(slice(a, a + w)), 0.0, A.mult, A.max))
+        return v(V.tensor_tensor_scan(T.tab[:, falling(to, w)], m, buf(falling(a, w)), 0.0, A.mult, A.max))
 
     def high(i, r):
-        V.wait_ge(ss, r[0])
+        V.wait_ge(ss, r)
         V.wait_ge(gs, consts)
         for k in range(TOP, LOW - 1, -1):
             for side in (0, 1):
                 if (k, side) not in PACK:
-                    scan(i, k, side, T.tab, TS * i + 1 + side * (COLS - width(k, side)))
+                    scan(i, k, side, lambda c: T.tab[:, c], TS * i + 1 + side * (COLS - width(k, side)), width(k, side), MK[k])
 
     def low(i, ready):
-        for key in PACK:
-            V.wait_ge(*ready[key])
-            last = scan(i, key[0], key[1], T.pk, packed(i, key))
+        last = []
+        for side in (0, 1):
+            run, w = RUNS[side], 128 * len(RUNS[side])
+            for key in run:
+                V.wait_ge(*ready[key])
+            first = MK[run[0][0]]
+            last.append(scan(i, run[0][0], side, lambda c: T.pk[:, i, c], packed(run[0]), w, first if side else first + 128 - w))
         return last
 
     def half_x(k):
@@ -251,57 +259,68 @@ def rank_program(g, core, T, topo):
     half_x(0)
     V.wait_ge(T.sem.la0, 16)
     z0 = [half_z(0, v(V.quantize_mx(T.qa[:, 0:128], T.sa[:, 0:128], T["at"][:, 0:512])))]
-    V.wait_ge(ss, floored)
-    v(V.tensor_tensor(T.dif[:], T.tj[:, PL * LW:2 * PL * LW], T.tj[:, 0:PL * LW], A.is_gt))
-    V.wait_ge(vs, edges)
-    d = v(V.tensor_tensor(T.dlow[:], T.edge[:, 2 * LW:4 * LW], T.edge[:, 0:2 * LW], A.is_gt))
-    z0.append(half_z(1, half_x(1)))
-    V.wait_ge(vs, d)
-    V.wait_ge(ss, cands)
-    for a in (0, PL * LW):
-        picked = v(V.tensor_tensor_scan(T.pick[:, a:a + PL * LW], T.dif[:], T.cand[:, a:a + PL * LW], 0.0, A.mult, A.max))
-    z1 = product_a(1)
-    V.wait_ge(vs, picked)
-    b = v(V.tensor_tensor(T.base[:], T.pick[:, PL - 1::PL], T.dlow[:], A.mult))
-    S.wait_ge(ts, z0[0])
-    s(S.activation(T.tab[:, 1:129], bank(0, 128), F.Relu, scale=0.05))
-    s(S.activation(T.h0[:, 0:2], bank(0, 128), F.Relu, scale=0.05))
-    S.wait_ge(ts, z0[1])
-    r0 = (s(S.activation(T.tab[:, 129:257], bank(4, 128), F.Relu, scale=0.05)),
-          s(S.activation(T.h0[:, 2:4], bank(4, 128), F.Relu, scale=0.05)))
-    r1 = result(1, z1)
-    p0 = pack(0, r0)
-    p1 = pack(1, r1)
-    high(0, r0)
-    V.wait_ge(vs, b)
-    offs = v(V.tensor_tensor(T.off[:], T.base[:], T.lr[:, LW:3 * LW], A.add))
-    r2 = result(2, product_a(2))
-    p2 = pack(2, r2)
-    high(1, r1)
-    w0 = low(0, p0)
-    r3 = result(3, product_a(3))
-    p3 = pack(3, r3)
-    high(2, r2)
-    w1 = low(1, p1)
-    high(3, r3)
-    w2 = low(2, p2)
-    w3 = low(3, p3)
+    zs, hs, cs, ps, whole = {}, {}, {}, [{}, {}, {}, {}], {}
+    for step in ORDER.split():
+        what, i = step[0], int(step[1])
+        if what == "x":
+            z0.append(half_z(1, half_x(1)))
+        elif what == "e":
+            S.wait_ge(ts, z0[i])
+            hs[0] = s(S.activation(T.tab[:, 1 + 128 * i:129 + 128 * i], bank(4 * i, 128), F.Relu, scale=0.05))
+        elif what == "f":
+            cs[0] = s(S.activation(T.h0[:, 2 * i:2 * i + 2], bank(4 * i, 128), F.Relu, scale=0.05))
+        elif what == "z":
+            zs[i] = product_a(i)
+        elif what == "h":
+            hs[i] = relu(T.tab[:, TS * i + 1:TS * i + 1 + COLS], i, zs[i])
+        elif what == "c":
+            cs[i] = relu(T["h%d" % i][:], i, zs[i])
+        elif what == "p":
+            for key in list(PACK)[len(ps[i]):int(step[2:] or len(PACK))]:
+                ps[i][key] = pack(i, key, cs[i])
+        elif what == "u":
+            high(i, hs[i])
+        elif what == "l":
+            whole[i] = low(i, ps[i])
+        elif i == 0:
+            V.wait_ge(vs, edges)
+            b = v(V.tensor_tensor(T.dlow[:], T.edge[:, 2 * LW:4 * LW], T.edge[:, 0:2 * LW], A.is_gt))
+        elif i == 1:
+            V.wait_ge(vs, b)
+            V.wait_ge(ss, cands)
+            for a in (0, PL * LW):
+                b = v(V.tensor_tensor_scan(T.pick[:, a:a + PL * LW], T.dif[:], T.cand[:, a:a + PL * LW], 0.0, A.mult, A.max))
+        elif i == 2:
+            V.wait_ge(vs, b)
+            b = v(V.tensor_tensor(T.base[:], T.pick[:, PL - 1::PL], T.dlow[:], A.mult))
+        else:
+            V.wait_ge(vs, b)
+            offs = v(V.tensor_tensor(T.off[:], T.base[:], T.lr[:, LW:3 * LW], A.add))
 
-    def left(j):
+    Y.wait_ge(vs, offs)
+    for side in (0, 1):
+        o = LW * side + CAPP * group[0][0] // 16
+        Y.dma_start(T.off0[:, LW * side:LW * side + CAPP // 16], T.off[:, o:o + CAPP // 16]).then_inc(T.sem.lof, 16)
+    S.wait_ge(T.sem.lof, 32)
+    for k in range(8):
+        Y.dma_start(T.lp[16 * k:16 * k + 16, 0:16], T.pf[:]).then_inc(T.sem.lpl, 16)
+        Y.dma_start(T.lp[16 * k:16 * k + 16, 16:32], T.pg[:]).then_inc(T.sem.lpl, 16)
+
+    def left(j, i):
         k, w, o = span[j]
-        done = []
-        for i, c in enumerate((w0, w1, w2, w3)):
-            S.wait_ge(vs, max(c, offs))
-            done.append(s(S.activation(T.left[:, PW * i + k:PW * i + k + w],
-                                       T.tab[:, TS * i:TS * i + TW].indirect(T.off[:, LW + o:LW + o + w // 16]), F.Copy)))
-        return done
+        off = T.off if j else T.off0
+        S.wait_ge(vs, max(whole[i][0], offs))
+        return s(S.activation(T.left[:, PW * i + k:PW * i + k + w],
+                              T.tab[:, TS * i:TS * i + TB[LOW, 1]].indirect(off[:, LW + o:LW + o + w // 16]), F.Copy))
 
     def right(j, results):
         k, w, o = span[j]
+        off = T.off if j else T.off0
         for i in results:
-            V.wait_ge(ss, lefts[j][i])
+            V.wait_ge(ss, lefts[j, i])
+            V.wait_ge(vs, whole[i][1])
             full = v(V.tensor_tensor(T.pt[:, 4 * k + i:4 * (k + w):4],
-                                     T.tab[:, TS * i:TS * i + TW].indirect(T.off[:, o:o + w // 16]),
+                                     T.tab[:, TS * i:TS * i + TW].indirect(off[:, o:o + w // 16]),
                                      T.left[:, PW * i + k:PW * i + k + w], A.max))
         return full
 
@@ -332,11 +351,10 @@ def rank_program(g, core, T, topo):
             g.remote_dma_fused(tr, local_sem=T.sem.sent)
         return 2 * w * nr
 
-    lefts = [left(j) for j in range(NG + 1)]
+    lefts = {(j, i): left(j, i) for j in range(NG + 1) for i in range(4)}
     sent = 0
-    sent = send(0, quantise(0, right(0, [0, 1, 2, 3])))
-    right(1, [0])
-    for j in range(1, NG):
+    right(0, [0])
+    for j in range(NG):
         full = right(j, [1, 2, 3])
         right(j + 1, [0])
         sent = sent + send(j, quantise(j, full))
@@ -364,7 +382,7 @@ def rank_program(g, core, T, topo):
         return cv, cu
 
     PE.wait_ge(vs, quv)
-    PE.wait_ge(ss, lefts[NG][3])
+    PE.wait_ge(ss, lefts[NG, 3])
     PE.wait_ge(T.sem.got0, 8)
     PE.wait_ge(T.sem.got1, 16)
     products(6, T.lc, T.ls, 0, land[2], [(land[0], 0), (land[1], 1)])
@@ -379,15 +397,14 @@ def rank_program(g, core, T, topo):
     S.wait_ge(ss, cv)
     V.wait_ge(vs, cu)
     done = []
-    for k in range(2):
-        c = slice(128 * k, 128 * k + 128)
-        f = s(S.activation(T.first[:, c], T.zv[:, 0:1 + SL].indirect(T.offp[:, 8 * k:8 * k + 8]), F.Copy))
+    for a, b in ((0, CUT), (CUT, P)):
+        f = s(S.activation(T.first[:, a:b], T.zv[:, 0:1 + SL].indirect(T.offp[:, a // 16:b // 16]), F.Copy))
         V.wait_ge(ss, f)
-        done.append(v(V.tensor_tensor(T.yt[:, c], T.zu[:, 0:1 + SL].indirect(T.offp[:, 16 + 8 * k:24 + 8 * k]), T.first[:, c], A.add)))
+        done.append(v(V.tensor_tensor(T.yt[:, a:b], T.zu[:, 0:1 + SL].indirect(T.offp[:, 16 + a // 16:16 + b // 16]), T.first[:, a:b], A.add)))
     Y.wait_ge(vs, done[0])
-    Y.dma_start(T.y[:, 0:128], T.yt[:, 0:128]).then_inc(T.sem.st0, 16)
+    Y.dma_start(T.y[:, 0:CUT], T.yt[:, 0:CUT]).then_inc(T.sem.st0, 16)
     S.wait_ge(vs, done[1])
-    S.dma_start(T.y[:, 128:256], T.yt[:, 128:256]).then_inc(T.sem.st1, 16)
+    S.dma_start(T.y[:, CUT:P], T.yt[:, CUT:P]).then_inc(T.sem.st1, 16)
     g.wait_ge(T.sem.sent, sent)
     Y.wait_ge(T.sem.st0, 16)
     S.wait_ge(T.sem.st1, 16)

@@ -9,9 +9,11 @@ RUN = 128
 PW = 480
 LOW, TOP = 2, 7
 PL = TOP - LOW + 1
-PACK = {(3, 0): "gggg", (3, 1): "gggg", (4, 0): "ssss", (5, 0): "ssss", (4, 1): "ssss", (5, 1): "ssss"}
-ORDER = "o0 x1 o1 z1 o2 e0 e1 f0 f1 h1 c1 u0 z2 o3 p0 h2 c2 u1 z3 p1 h3 c3 l0 u2 p2 l1 u3 p3 l2 l3"
-CUT = 128
+BY_G, BY_S = [(3, 0), (3, 1)], [(4, 0), (5, 0), (4, 1), (5, 1)]
+PACK = BY_G + BY_S
+ORDER = ("n0 n1 x1 d0 z1 e0 f0 o0 o1 e1 z2 f1 u0 z3 h1 g0 o2 c1 c2 u1 o3 h2 p0 p0 g1 c3 h3 p0 p0 p1 p1 u2 b0 p1 g2 u3 r0 r1 g3 "
+         "b1 b2 b3 p1 r2 r3")
+CUT = (32, 128)
 ZW = 392
 
 
@@ -58,10 +60,8 @@ SCRATCH = {
     "sa": ("sbuf", [128, 512], "uint8"),
     "quv": ("sbuf", [128, 256], "float8_e4m3fn_x4"),
     "suv": ("sbuf", [128, 256], "uint8"),
-    "h0": ("sbuf", [128, 4, 4, 4, 4], "bfloat16"),
-    "h1": ("sbuf", [128, 4, 4, 4, 4], "bfloat16"),
-    "h2": ("sbuf", [128, 4, 4, 4, 4], "bfloat16"),
-    "h3": ("sbuf", [128, 4, 4, 4, 4], "bfloat16"),
+    "h0": ("sbuf", [128, 8, 4, 4, 4], "bfloat16"),
+    "h1": ("sbuf", [128, 8, 4, 4, 4], "bfloat16"),
     "tab": ("sbuf", [128, 4 * TS], "bfloat16"),
     "mask": ("sbuf", [128, MW], "bfloat16"),
     "pk": ("sbuf", [128, 4, len(PACK) * 128], "bfloat16"),
@@ -84,8 +84,8 @@ SEMAPHORES = ["vs", "ss", "ts", "gs", "lst", "lx0", "lx1", "la0", "la1", "la2", 
               "sent", "st0", "st1"]
 
 
-def half(h, k, bit):
-    ix = [slice(None)] * 5
+def half(h, top, k, bit):
+    ix = [slice(None), top] + [slice(None)] * 3
     ix[4 - k // 2] = slice(2 * bit, 2 * bit + 2) if k % 2 else slice(bit, None, 2)
     return h[tuple(ix)]
 
@@ -148,6 +148,9 @@ def rank_program(g, core, T, topo):
         (Y if i else S).dma_start(T["at"][:, 512 * i:512 * i + 512], T.a[:, 512 * i:512 * i + 512]).then_inc(T.sem["la%d" % i], 16)
     Y.dma_start(T.uvt[:, 0:512], T.u[:]).then_inc(T.sem.luv, 16)
     Y.dma_start(T.uvt[:, 512:1024], T.v[:]).then_inc(T.sem.luv, 16)
+    for k in range(8):
+        Y.dma_start(T.lp[16 * k:16 * k + 16, 0:16], T.pf[:]).then_inc(T.sem.lpl, 16)
+        Y.dma_start(T.lp[16 * k:16 * k + 16, 16:32], T.pg[:]).then_inc(T.sem.lpl, 16)
 
     def cand(k, side):
         a = PL * LW * (1 - side)
@@ -184,22 +187,21 @@ def rank_program(g, core, T, topo):
         return 128.5 + (shift - 0.5) * 2.0 ** -j
 
     S.wait_ge(vs, lists)
-    V.wait_ge(vs, lists)
-    for j in range(LOW + 1, TOP + 1):
-        if j < TOP - 1:
-            floored = s(S.activation(floors(j, None), T.lr[:, 0:2 * LW], F.Identity, bias=bias(j, 0), scale=2.0 ** -j))
-        else:
-            upper = v(V.tensor_scalar(floors(j, None), T.lr[:, 0:2 * LW], 2.0 ** -j, bias(j, 0), A.mult, A.add))
-    for a, b, c, shift in ((0, 1, 0, -1), (1, 3, 0, 0), (3, 4, 1, 1)):
-        edges = v(V.tensor_scalar(T.edge[:, LW * a:LW * b], T.lr[:, LW * c:LW * (c + b - a)], 2.0 ** -LOW, bias(LOW, shift),
-                                  A.mult, A.add))
-    V.wait_ge(ss, floored)
-    V.wait_ge(vs, upper)
-    v(V.tensor_tensor(T.dif[:], T.tj[:, PL * LW:2 * PL * LW], T.tj[:, 0:PL * LW], A.is_gt))
-    S.wait_ge(ss, floored)
-    for k, side in sorted(PACK):
-        w = 2.0 ** (k - 1)
-        cands = s(S.activation(cand(k, side), floors(k, 1), F.Identity, bias=TB[k, side] - 1 + (130 - 2 * side) * w, scale=-w))
+    floored = [s(S.activation(floors(j, None), T.lr[:, 0:2 * LW], F.Identity, bias=bias(j, 0), scale=2.0 ** -j))
+               for j in range(LOW + 1, TOP + 1)]
+
+    def blocks():
+        for a, b, c, shift in ((0, 1, 0, -1), (1, 3, 0, 0), (3, 4, 1, 1)):
+            last = s(S.activation(T.edge[:, LW * a:LW * b], T.lr[:, LW * c:LW * (c + b - a)], F.Identity, bias=bias(LOW, shift),
+                                  scale=2.0 ** -LOW))
+        return last
+
+    def candidates():
+        S.wait_ge(ss, floored[max(PACK)[0] - LOW - 1])
+        for k, side in sorted(PACK):
+            w = 2.0 ** (k - 1)
+            last = s(S.activation(cand(k, side), floors(k, 1), F.Identity, bias=TB[k, side] - 1 + (130 - 2 * side) * w, scale=-w))
+        return last
 
     def product_a(i):
         V.wait_ge(T.sem["la%d" % i], 16)
@@ -215,13 +217,15 @@ def rank_program(g, core, T, topo):
         S.wait_ge(ts, z)
         return s(S.activation(out, bank(i, COLS), F.Relu, scale=0.05))
 
-    def pack(i, key, r):
-        h, to = T["h%d" % i], T.pk[:, i, packed(key):packed(key) + 128]
-        if PACK[key][i] == "s":
-            S.wait_ge(ss, r)
-            return ss, s(S.activation(to, half(h, *key), F.Copy))
+    def pack_s(pair, key, r):
+        S.wait_ge(ss, r)
+        to = T.pk[:, 2 * pair:2 * pair + 2, packed(key):packed(key) + 128]
+        return ss, s(S.activation(to, half(T["h%d" % pair], slice(None), *key), F.Copy))
+
+    def pack_g(i, key, r):
         g.wait_ge(ss, r)
-        return gs, gp(g.affine_select(to, half(h, *key), [[0, 128]], A.is_equal, 0.0, 0, 0))
+        src = half(T["h%d" % (i // 2)], slice(4 * (i % 2), 4 * (i % 2) + 4), *key)
+        return gs, gp(g.affine_select(T.pk[:, i, packed(key):packed(key) + 128], src, [[0, 128]], A.is_equal, 0.0, 0, 0))
 
     def scan(i, k, side, buf, a, w, m):
         to, m = TS * i + TB[k, side], T.mask[:, m:m + w]
@@ -237,15 +241,12 @@ def rank_program(g, core, T, topo):
                 if (k, side) not in PACK:
                     scan(i, k, side, lambda c: T.tab[:, c], TS * i + 1 + side * (COLS - width(k, side)), width(k, side), MK[k])
 
-    def low(i, ready):
-        last = []
-        for side in (0, 1):
-            run, w = RUNS[side], 128 * len(RUNS[side])
-            for key in run:
-                V.wait_ge(*ready[key])
-            first = MK[run[0][0]]
-            last.append(scan(i, run[0][0], side, lambda c: T.pk[:, i, c], packed(run[0]), w, first if side else first + 128 - w))
-        return last
+    def low(i, side, ready):
+        run, w = RUNS[side], 128 * len(RUNS[side])
+        for key in run:
+            V.wait_ge(*ready[key])
+        first = MK[run[0][0]]
+        return scan(i, run[0][0], side, lambda c: T.pk[:, i, c], packed(run[0]), w, first if side else first + 128 - w)
 
     def half_x(k):
         V.wait_ge(T.sem["lx%d" % k], 16)
@@ -274,24 +275,34 @@ def rank_program(g, core, T, topo):
         elif what == "h":
             hs[i] = relu(T.tab[:, TS * i + 1:TS * i + 1 + COLS], i, zs[i])
         elif what == "c":
-            cs[i] = relu(T["h%d" % i][:], i, zs[i])
+            cs[i] = relu(T["h%d" % (i // 2)][:, 4 * (i % 2):4 * (i % 2) + 4], i, zs[i])
+        elif what == "g":
+            for key in BY_G:
+                ps[i][key] = pack_g(i, key, cs[i])
         elif what == "p":
-            for key in list(PACK)[len(ps[i]):int(step[2:] or len(PACK))]:
-                ps[i][key] = pack(i, key, cs[i])
+            key = [key for key in BY_S if key not in ps[2 * i]][0]
+            ps[2 * i][key] = ps[2 * i + 1][key] = pack_s(i, key, max(cs[2 * i], cs[2 * i + 1]))
         elif what == "u":
             high(i, hs[i])
-        elif what == "l":
-            whole[i] = low(i, ps[i])
+        elif what in "br":
+            whole[i, "br".index(what)] = low(i, "br".index(what), ps[i])
+        elif step == "n0":
+            edges = blocks()
+        elif step == "n1":
+            cands = candidates()
+        elif what == "d":
+            V.wait_ge(ss, floored[-1])
+            differ = v(V.tensor_tensor(T.dif[:], T.tj[:, PL * LW:2 * PL * LW], T.tj[:, 0:PL * LW], A.is_gt))
         elif i == 0:
-            V.wait_ge(vs, edges)
-            b = v(V.tensor_tensor(T.dlow[:], T.edge[:, 2 * LW:4 * LW], T.edge[:, 0:2 * LW], A.is_gt))
+            V.wait_ge(ss, edges)
+            lowest = v(V.tensor_tensor(T.dlow[:], T.edge[:, 2 * LW:4 * LW], T.edge[:, 0:2 * LW], A.is_gt))
         elif i == 1:
-            V.wait_ge(vs, b)
+            V.wait_ge(vs, differ)
             V.wait_ge(ss, cands)
             for a in (0, PL * LW):
                 b = v(V.tensor_tensor_scan(T.pick[:, a:a + PL * LW], T.dif[:], T.cand[:, a:a + PL * LW], 0.0, A.mult, A.max))
         elif i == 2:
-            V.wait_ge(vs, b)
+            V.wait_ge(vs, max(b, lowest))
             b = v(V.tensor_tensor(T.base[:], T.pick[:, PL - 1::PL], T.dlow[:], A.mult))
         else:
             V.wait_ge(vs, b)
@@ -302,14 +313,11 @@ def rank_program(g, core, T, topo):
         o = LW * side + CAPP * group[0][0] // 16
         Y.dma_start(T.off0[:, LW * side:LW * side + CAPP // 16], T.off[:, o:o + CAPP // 16]).then_inc(T.sem.lof, 16)
     S.wait_ge(T.sem.lof, 32)
-    for k in range(8):
-        Y.dma_start(T.lp[16 * k:16 * k + 16, 0:16], T.pf[:]).then_inc(T.sem.lpl, 16)
-        Y.dma_start(T.lp[16 * k:16 * k + 16, 16:32], T.pg[:]).then_inc(T.sem.lpl, 16)
 
     def left(j, i):
         k, w, o = span[j]
         off = T.off if j else T.off0
-        S.wait_ge(vs, max(whole[i][0], offs))
+        S.wait_ge(vs, max(whole[i, 0], offs))
         return s(S.activation(T.left[:, PW * i + k:PW * i + k + w],
                               T.tab[:, TS * i:TS * i + TB[LOW, 1]].indirect(off[:, LW + o:LW + o + w // 16]), F.Copy))
 
@@ -318,7 +326,7 @@ def rank_program(g, core, T, topo):
         off = T.off if j else T.off0
         for i in results:
             V.wait_ge(ss, lefts[j, i])
-            V.wait_ge(vs, whole[i][1])
+            V.wait_ge(vs, whole[i, 1])
             full = v(V.tensor_tensor(T.pt[:, 4 * k + i:4 * (k + w):4],
                                      T.tab[:, TS * i:TS * i + TW].indirect(off[:, o:o + w // 16]),
                                      T.left[:, PW * i + k:PW * i + k + w], A.max))
@@ -329,42 +337,46 @@ def rank_program(g, core, T, topo):
         V.wait_ge(vs, full)
         return v(V.quantize_mx(T["q%d" % j][:], T["s%d" % j][:], T.pt[:, 4 * (k + w - RUN):4 * (k + w)]))
 
-    def send(j, q):
+    def transfer(j, i, codes, share):
         r0, nr = group[j]
+        d = T.cores[r0 + i]
+        rid, pid = topo.addr(d, core)
+        to, c = land[j] + CAPP * (rank - groups(r0 + i)[j][0]), RUN - CAPP * (nr - i)
+        if codes:
+            a, b = T["q%d" % j][:, c:c + CAPP].bitcast(dt.uint8), T.lc[:, to:to + CAPP].bitcast(dt.uint8)
+        else:
+            a, b = T["s%d" % j][:, c:c + CAPP], T.ls[:, to:to + CAPP]
+        e = topo.engines(core, d)[share]
+        return RemoteDMATransfer(dst_ids=[DstId(rid=rid, pnc=pid)], dma_engine_mask=sum(1 << x for x in e),
+                                 remote_sem=T.sem["got%d" % j], src=a, dst=b), len(e)
+
+    def send(j, q):
+        k = len(topo.engines(core, T.cores[group[j][0]])) // 2
+        calls = [[(0, codes, slice(0, k)), (1, codes, slice(k, None))] for codes in (True, False)]
+        if group[j][1] == 1:
+            calls = [[(0, True, slice(0, None, 2))], [(0, False, slice(1, None, 2))]]
         g.wait_ge(vs, q)
-        for src, dst, codes in (("q%d" % j, "lc", True), ("s%d" % j, "ls", False)):
-            tr = []
-            for i in range(nr):
-                d = T.cores[r0 + i]
-                rid, pid = topo.addr(d, core)
-                to = land[j] + CAPP * (rank - groups(r0 + i)[j][0])
-                c = RUN - CAPP * (nr - i)
-                a, b = T[src][:, c:c + CAPP], T[dst][:, to:to + CAPP]
-                if codes:
-                    a, b = a.bitcast(dt.uint8), b.bitcast(dt.uint8)
-                e = topo.engines(core, d)
-                if j == 0:
-                    e = e[0::2] if codes else e[1::2]
-                w = len(e) // nr
-                tr.append(RemoteDMATransfer(dst_ids=[DstId(rid=rid, pnc=pid)], dma_engine_mask=sum(1 << x for x in e[w * i:w * i + w]),
-                                            remote_sem=T.sem["got%d" % j], src=a, dst=b))
-            g.remote_dma_fused(tr, local_sem=T.sem.sent)
-        return 2 * w * nr
+        count = 0
+        for call in calls:
+            tr = [transfer(j, *x) for x in call]
+            g.remote_dma_fused([x for x, w in tr], local_sem=T.sem.sent)
+            count += sum(w for x, w in tr)
+        return count
 
     lefts = {(j, i): left(j, i) for j in range(NG + 1) for i in range(4)}
     sent = 0
     right(0, [0])
     for j in range(NG):
         full = right(j, [1, 2, 3])
+        if j == NG - 1:
+            V.wait_ge(T.sem.lpl, 256)
+            places = v(V.tensor_scalar(T.offp[:], T.lp[:], 1, None, A.add))
         right(j + 1, [0])
         sent = sent + send(j, quantise(j, full))
 
     V.wait_ge(T.sem.luv, 32)
     quv = v(V.quantize_mx(T.quv[:], T.suv[:], T.uvt[:]))
-    full = right(NG, [1, 2, 3])
-    V.wait_ge(T.sem.lpl, 256)
-    places = v(V.tensor_scalar(T.offp[:], T.lp[:], 1, None, A.add))
-    own = quantise(NG, full)
+    own = quantise(NG, right(NG, [1, 2, 3]))
 
     def products(bv, codes, scales, a, b, parts, last=False):
         cu = None
@@ -396,15 +408,19 @@ def rank_program(g, core, T, topo):
     S.wait_ge(vs, places)
     S.wait_ge(ss, cv)
     V.wait_ge(vs, cu)
+    V.wait_ge(ss, cv)
+    parts, firsts = list(zip((0,) + CUT, CUT + (P,))), []
+    for k, (a, b) in enumerate(parts):
+        win = T.zv[:, 0:1 + SL].indirect(T.offp[:, a // 16:b // 16])
+        firsts.append((vs, v(V.tensor_copy(T.first[:, a:b], win))) if k == 1 else (ss, s(S.activation(T.first[:, a:b], win, F.Copy))))
     done = []
-    for a, b in ((0, CUT), (CUT, P)):
-        f = s(S.activation(T.first[:, a:b], T.zv[:, 0:1 + SL].indirect(T.offp[:, a // 16:b // 16]), F.Copy))
-        V.wait_ge(ss, f)
+    for (a, b), f in zip(parts, firsts):
+        V.wait_ge(*f)
         done.append(v(V.tensor_tensor(T.yt[:, a:b], T.zu[:, 0:1 + SL].indirect(T.offp[:, 16 + a // 16:16 + b // 16]), T.first[:, a:b], A.add)))
-    Y.wait_ge(vs, done[0])
-    Y.dma_start(T.y[:, 0:CUT], T.yt[:, 0:CUT]).then_inc(T.sem.st0, 16)
-    S.wait_ge(vs, done[1])
-    S.dma_start(T.y[:, CUT:P], T.yt[:, CUT:P]).then_inc(T.sem.st1, 16)
+    Y.wait_ge(vs, done[1])
+    Y.dma_start(T.y[:, 0:CUT[1]], T.yt[:, 0:CUT[1]]).then_inc(T.sem.st0, 16)
+    S.wait_ge(vs, done[2])
+    S.dma_start(T.y[:, CUT[1]:P], T.yt[:, CUT[1]:P]).then_inc(T.sem.st1, 16)
     g.wait_ge(T.sem.sent, sent)
     Y.wait_ge(T.sem.st0, 16)
     S.wait_ge(T.sem.st1, 16)

from concourse.bass import DstId, RemoteDMATransfer
from concourse.mybir import dt, AluOpType, ActivationFunctionType

N, CAPP, COLS, P = 8, 48, 256, 256
SL = N * CAPP
LW = SL // 16
LAND = (N - 1) * CAPP
RUN = 128
PW = 480
LOW, TOP = 2, 7
PL = TOP - LOW + 1
BY_G, BY_S = [(3, 0), (3, 1)], [(4, 0), (5, 0), (4, 1), (5, 1)]
PACK = BY_G + BY_S
ORDER = ("n0 n1 x1 d0 z1 e0 f0 o0 o1 e1 z2 f1 u0 z3 h1 g0 o2 c1 c2 u1 o3 h2 p0 p0 g1 c3 h3 p0 p0 p1 p1 u2 b0 p1 g2 u3 r0 r1 g3 "
         "b1 b2 b3 p1 r2 r3")
CUT = (32, 128)
ZW = 392


def width(k, side):
    return COLS // 2 if (k, side) in PACK else COLS if k == LOW else COLS - (1 << k)


def layout():
    tb, at = {}, 1 + COLS
    for side in (0, 1):
        for k in range(LOW, TOP + 1):
            tb[k, side], at = at, at + width(k, side)
    m, am = [], 0
    for k in [LOW] + list(range(TOP, LOW, -1)) + [k for k, side in RUNS[1][1:]]:
        m.append((k, am, max(width(k, 0), width(k, 1))))
        am += m[-1][2]
    return tb, m, at, am


RUNS = [sorted(key for key in PACK if key[1] == side) for side in (0, 1)]
TB, MASKS, TW, MW = layout()
MK = {k: a for k, a, w in MASKS[::-1]}
TS = (TW + 15) // 16 * 16

SCRATCH = {
    "lol": ("sbuf", [128, 2 * LW], "int32"),
    "one": ("sbuf", [128, 2 * LW], "float32"),
    "lr": ("sbuf", [128, 3 * LW], "float32"),
    "tj": ("sbuf", [128, 2 * PL * LW], "bfloat16"),
    "edge": ("sbuf", [128, 4 * LW], "bfloat16"),
    "dif": ("sbuf", [128, PL * LW], "bfloat16"),
    "dlow": ("sbuf", [128, 2 * LW], "bfloat16"),
    "cand": ("sbuf", [128, 2 * PL * LW], "float32"),
    "pick": ("sbuf", [128, 2 * PL * LW], "float32"),
    "base": ("sbuf", [128, 2 * LW], "float32"),
    "off": ("sbuf", [128, 2 * LW], "uint16"),
    "off0": ("sbuf", [128, 2 * LW], "uint16"),
    "xt": ("sbuf", [128, 1024], "bfloat16"),
    "at": ("sbuf", [128, 2048], "bfloat16"),
    "uvt": ("sbuf", [128, 1024], "bfloat16"),
    "qx": ("sbuf", [128, 256], "float8_e4m3fn_x4"),
    "sx": ("sbuf", [128, 256], "uint8"),
    "qa": ("sbuf", [128, 512], "float8_e4m3fn_x4"),
    "sa": ("sbuf", [128, 512], "uint8"),
    "quv": ("sbuf", [128, 256], "float8_e4m3fn_x4"),
    "suv": ("sbuf", [128, 256], "uint8"),
    "h0": ("sbuf", [128, 8, 4, 4, 4], "bfloat16"),
    "h1": ("sbuf", [128, 8, 4, 4, 4], "bfloat16"),
    "tab": ("sbuf", [128, 4 * TS], "bfloat16"),
    "mask": ("sbuf", [128, MW], "bfloat16"),
    "pk": ("sbuf", [128, 4, len(PACK) * 128], "bfloat16"),
    "left": ("sbuf", [128, 4 * PW], "bfloat16"),
    "pt": ("sbuf", [128, 4 * PW], "bfloat16"),
    "lc": ("sbuf", [128, LAND], "float8_e4m3fn_x4"),
    "ls": ("sbuf", [128, LAND], "uint8"),
    "lp": ("sbuf", [128, 32], "int32"),
    "offp": ("sbuf", [128, 32], "uint16"),
    "zv": ("sbuf", [128, ZW], "float32"),
    "zu": ("sbuf", [128, ZW], "float32"),
    "first": ("sbuf", [128, P], "float32"),
    "yt": ("sbuf", [128, P], "float32"),
    "ps": ("psum", [128, 4096], "float32"),
}
for _j in range(5):
    SCRATCH["q%d" % _j] = ("sbuf", [128, RUN], "float8_e4m3fn_x4")
    SCRATCH["s%d" % _j] = ("sbuf", [128, RUN], "uint8")
SEMAPHORES = ["vs", "ss", "ts", "gs", "lst", "lx0", "lx1", "la0", "la1", "la2", "la3", "luv", "lpl", "lof", "got0", "got1", "got2", "got3",
              "sent", "st0", "st1"]


def half(h, top, k, bit):
    ix = [slice(None), top] + [slice(None)] * 3
    ix[4 - k // 2] = slice(2 * bit, 2 * bit + 2) if k % 2 else slice(bit, None, 2)
    return h[tuple(ix)]


def falling(a, w):
    return slice(a + w - 1, a - 1 if a else None, -1)


def groups(rank):
    p = rank // 2
    return (rank ^ 1, 1), (2 * (p ^ 2), 2), (2 * (p ^ 3), 2), (2 * (p ^ 1), 2), (rank, 1)


def rank_program(g, core, T, topo):
    rank = T.rank_of(core)
    if rank is None:
        return
    V, S, PE, Y = g.vector, g.scalar, g.tensor, g.sync
    A, F = AluOpType, ActivationFunctionType
    vs, ss, ts, gs = T.sem.vs, T.sem.ss, T.sem.ts, T.sem.gs
    group = groups(rank)
    NG = len(group) - 1
    n = {"v": 0, "s": 0, "t": 0, "g": 0}

    def v(i):
        n["v"] += 1
        i.then_inc(vs, 1)
        return n["v"]

    def s(i):
        n["s"] += 1
        i.then_inc(ss, 1)
        return n["s"]

    def t(i):
        n["t"] += 1
        i.then_inc(ts, 1)
        return n["t"]

    def gp(i):
        n["g"] += 1
        i.then_inc(gs, 1)
        return n["g"]

    def bank(b, w):
        return T.ps[:, 512 * b:512 * b + w]

    span, land, at = [], [0], RUN - CAPP * group[0][1]
    for r0, nr in group:
        o = CAPP * r0 // 16 if span else 0
        span.append((at, CAPP * nr + 16 * (o % 2), o - o % 2))
        at += span[-1][1]
        land.append(land[-1] + CAPP * nr)

    S.dma_start(T.lol[:, 0:LW], T.lo[:]).then_inc(T.sem.lst, 16)
    Y.dma_start(T.lol[:, LW:2 * LW], T.ln[:]).then_inc(T.sem.lst, 16)
    for i in range(4):
        if i < 2:
            Y.dma_start(T.xt[:, 512 * i:512 * i + 512], T.x[:, 512 * i:512 * i + 512]).then_inc(T.sem["lx%d" % i], 16)
        (Y if i else S).dma_start(T["at"][:, 512 * i:512 * i + 512], T.a[:, 512 * i:512 * i + 512]).then_inc(T.sem["la%d" % i], 16)
    Y.dma_start(T.uvt[:, 0:512], T.u[:]).then_inc(T.sem.luv, 16)
    Y.dma_start(T.uvt[:, 512:1024], T.v[:]).then_inc(T.sem.luv, 16)
    for k in range(8):
        Y.dma_start(T.lp[16 * k:16 * k + 16, 0:16], T.pf[:]).then_inc(T.sem.lpl, 16)
        Y.dma_start(T.lp[16 * k:16 * k + 16, 16:32], T.pg[:]).then_inc(T.sem.lpl, 16)

    def cand(k, side):
        a = PL * LW * (1 - side)
        return T.cand[:, a + TOP - k:a + PL * LW:PL]

    def floors(j, part):
        a, b = (0, 2) if part is None else (part, part + 1)
        return T.tj[:, PL * LW * a + TOP + 1 - j:PL * LW * b:PL]

    S.wait_ge(vs, v(V.memset(T.one[:], 1.0)))
    g.wait_ge(vs, v(V.memset(T.mask[:], 1.0)))

    def fill(ap, w, c):
        return s(S.activation(ap, T.one[:, 0:w], F.Identity, scale=float(c)))

    fill(T.tj[:, 0::PL], 2 * LW, 0)
    for k in range(LOW, TOP + 1):
        for side in (0, 1):
            if (k, side) not in PACK:
                fill(cand(k, side), LW, TB[k, side] - 1 - side * (COLS - width(k, side)))
    fill(T.tab[:, 0::TS], 4, 0)
    fill(T.zv[:, 0:1], 1, 0)
    fill(T.zu[:, 0:1], 1, 0)
    for k, a, w in MASKS:
        consts = gp(g.iota(T.mask[:, a:a + w:1 << k], [[0, w >> k]], 0, 0, allow_small_or_imprecise_dtypes=True))
    gp(g.iota(T.pt[:, 0:4 * span[0][0]], [[0, 4 * span[0][0]]], 0, 0, allow_small_or_imprecise_dtypes=True))

    V.wait_ge(T.sem.lst, 32)
    v(V.tensor_scalar(T.lr[:, 0:LW], T.lol[:, 0:LW], 1, None, A.add))
    lists = v(V.tensor_tensor(T.lr[:, LW:2 * LW], T.lol[:, 0:LW], T.lol[:, LW:2 * LW], A.add))
    v(V.tensor_scalar(T.lr[:, 2 * LW:3 * LW], T.lol[:, 0:LW], 1, None, A.add))

    def bias(j, shift):
        return 128.5 + (shift - 0.5) * 2.0 ** -j

    S.wait_ge(vs, lists)
    floored = [s(S.activation(floors(j, None), T.lr[:, 0:2 * LW], F.Identity, bias=bias(j, 0), scale=2.0 ** -j))
               for j in range(LOW + 1, TOP + 1)]

    def blocks():
        for a, b, c, shift in ((0, 1, 0, -1), (1, 3, 0, 0), (3, 4, 1, 1)):
            last = s(S.activation(T.edge[:, LW * a:LW * b], T.lr[:, LW * c:LW * (c + b - a)], F.Identity, bias=bias(LOW, shift),
                                  scale=2.0 ** -LOW))
        return last

    def candidates():
        S.wait_ge(ss, floored[max(PACK)[0] - LOW - 1])
        for k, side in sorted(PACK):
            w = 2.0 ** (k - 1)
            last = s(S.activation(cand(k, side), floors(k, 1), F.Identity, bias=TB[k, side] - 1 + (130 - 2 * side) * w, scale=-w))
        return last

    def product_a(i):
        V.wait_ge(T.sem["la%d" % i], 16)
        c = slice(128 * i, 128 * i + 128)
        q = v(V.quantize_mx(T.qa[:, c], T.sa[:, c], T["at"][:, 512 * i:512 * i + 512]))
        PE.wait_ge(vs, q)
        return t(PE.matmul_mx(bank(i, COLS), T.qa[:, c], T.sa[:, c], T.qx[:], T.sx[:], True, True))

    def packed(key):
        return 128 * (RUNS[0] + RUNS[1]).index(key)

    def relu(out, i, z):
        S.wait_ge(ts, z)
        return s(S.activation(out, bank(i, COLS), F.Relu, scale=0.05))

    def pack_s(pair, key, r):
        S.wait_ge(ss, r)
        to = T.pk[:, 2 * pair:2 * pair + 2, packed(key):packed(key) + 128]
        return ss, s(S.activation(to, half(T["h%d" % pair], slice(None), *key), F.Copy))

    def pack_g(i, key, r):
        g.wait_ge(ss, r)
        src = half(T["h%d" % (i // 2)], slice(4 * (i % 2), 4 * (i % 2) + 4), *key)
        return gs, gp(g.affine_select(T.pk[:, i, packed(key):packed(key) + 128], src, [[0, 128]], A.is_equal, 0.0, 0, 0))

    def scan(i, k, side, buf, a, w, m):
        to, m = TS * i + TB[k, side], T.mask[:, m:m + w]
        if side:
            return v(V.tensor_tensor_scan(T.tab[:, to:to + w], m, buf(slice(a, a + w)), 0.0, A.mult, A.max))
        return v(V.tensor_tensor_scan(T.tab[:, falling(to, w)], m, buf(falling(a, w)), 0.0, A.mult, A.max))

    def high(i, r):
        V.wait_ge(ss, r)
        V.wait_ge(gs, consts)
        for k in range(TOP, LOW - 1, -1):
            for side in (0, 1):
                if (k, side) not in PACK:
                    scan(i, k, side, lambda c: T.tab[:, c], TS * i + 1 + side * (COLS - width(k, side)), width(k, side), MK[k])

    def low(i, side, ready):
        run, w = RUNS[side], 128 * len(RUNS[side])
        for key in run:
            V.wait_ge(*ready[key])
        first = MK[run[0][0]]
        return scan(i, run[0][0], side, lambda c: T.pk[:, i, c], packed(run[0]), w, first if side else first + 128 - w)

    def half_x(k):
        V.wait_ge(T.sem["lx%d" % k], 16)
        return v(V.quantize_mx(T.qx[:, 128 * k:128 * k + 128], T.sx[:, 128 * k:128 * k + 128], T.xt[:, 512 * k:512 * k + 512]))

    def half_z(k, q):
        c = slice(128 * k, 128 * k + 128)
        PE.wait_ge(vs, q)
        return t(PE.matmul_mx(bank(4 * k, 128), T.qa[:, 0:128], T.sa[:, 0:128], T.qx[:, c], T.sx[:, c], True, True))

    half_x(0)
    V.wait_ge(T.sem.la0, 16)
    z0 = [half_z(0, v(V.quantize_mx(T.qa[:, 0:128], T.sa[:, 0:128], T["at"][:, 0:512])))]
    zs, hs, cs, ps, whole = {}, {}, {}, [{}, {}, {}, {}], {}
    for step in ORDER.split():
        what, i = step[0], int(step[1])
        if what == "x":
            z0.append(half_z(1, half_x(1)))
        elif what == "e":
            S.wait_ge(ts, z0[i])
            hs[0] = s(S.activation(T.tab[:, 1 + 128 * i:129 + 128 * i], bank(4 * i, 128), F.Relu, scale=0.05))
        elif what == "f":
            cs[0] = s(S.activation(T.h0[:, 2 * i:2 * i + 2], bank(4 * i, 128), F.Relu, scale=0.05))
        elif what == "z":
            zs[i] = product_a(i)
        elif what == "h":
            hs[i] = relu(T.tab[:, TS * i + 1:TS * i + 1 + COLS], i, zs[i])
        elif what == "c":
            cs[i] = relu(T["h%d" % (i // 2)][:, 4 * (i % 2):4 * (i % 2) + 4], i, zs[i])
        elif what == "g":
            for key in BY_G:
                ps[i][key] = pack_g(i, key, cs[i])
        elif what == "p":
            key = [key for key in BY_S if key not in ps[2 * i]][0]
            ps[2 * i][key] = ps[2 * i + 1][key] = pack_s(i, key, max(cs[2 * i], cs[2 * i + 1]))
        elif what == "u":
            high(i, hs[i])
        elif what in "br":
            whole[i, "br".index(what)] = low(i, "br".index(what), ps[i])
        elif step == "n0":
            edges = blocks()
        elif step == "n1":
            cands = candidates()
        elif what == "d":
            V.wait_ge(ss, floored[-1])
            differ = v(V.tensor_tensor(T.dif[:], T.tj[:, PL * LW:2 * PL * LW], T.tj[:, 0:PL * LW], A.is_gt))
        elif i == 0:
            V.wait_ge(ss, edges)
            lowest = v(V.tensor_tensor(T.dlow[:], T.edge[:, 2 * LW:4 * LW], T.edge[:, 0:2 * LW], A.is_gt))
        elif i == 1:
            V.wait_ge(vs, differ)
            V.wait_ge(ss, cands)
            for a in (0, PL * LW):
                b = v(V.tensor_tensor_scan(T.pick[:, a:a + PL * LW], T.dif[:], T.cand[:, a:a + PL * LW], 0.0, A.mult, A.max))
        elif i == 2:
            V.wait_ge(vs, max(b, lowest))
            b = v(V.tensor_tensor(T.base[:], T.pick[:, PL - 1::PL], T.dlow[:], A.mult))
        else:
            V.wait_ge(vs, b)
            offs = v(V.tensor_tensor(T.off[:], T.base[:], T.lr[:, LW:3 * LW], A.add))

    Y.wait_ge(vs, offs)
    for side in (0, 1):
        o = LW * side + CAPP * group[0][0] // 16
        Y.dma_start(T.off0[:, LW * side:LW * side + CAPP // 16], T.off[:, o:o + CAPP // 16]).then_inc(T.sem.lof, 16)
    S.wait_ge(T.sem.lof, 32)

    def left(j, i):
        k, w, o = span[j]
        off = T.off if j else T.off0
        S.wait_ge(vs, max(whole[i, 0], offs))
        return s(S.activation(T.left[:, PW * i + k:PW * i + k + w],
                              T.tab[:, TS * i:TS * i + TB[LOW, 1]].indirect(off[:, LW + o:LW + o + w // 16]), F.Copy))

    def right(j, results):
        k, w, o = span[j]
        off = T.off if j else T.off0
        for i in results:
            V.wait_ge(ss, lefts[j, i])
            V.wait_ge(vs, whole[i, 1])
            full = v(V.tensor_tensor(T.pt[:, 4 * k + i:4 * (k + w):4],
                                     T.tab[:, TS * i:TS * i + TW].indirect(off[:, o:o + w // 16]),
                                     T.left[:, PW * i + k:PW * i + k + w], A.max))
        return full

    def quantise(j, full):
        k, w, o = span[j]
        V.wait_ge(vs, full)
        return v(V.quantize_mx(T["q%d" % j][:], T["s%d" % j][:], T.pt[:, 4 * (k + w - RUN):4 * (k + w)]))

    def transfer(j, i, codes, share):
        r0, nr = group[j]
        d = T.cores[r0 + i]
        rid, pid = topo.addr(d, core)
        to, c = land[j] + CAPP * (rank - groups(r0 + i)[j][0]), RUN - CAPP * (nr - i)
        if codes:
            a, b = T["q%d" % j][:, c:c + CAPP].bitcast(dt.uint8), T.lc[:, to:to + CAPP].bitcast(dt.uint8)
        else:
            a, b = T["s%d" % j][:, c:c + CAPP], T.ls[:, to:to + CAPP]
        e = topo.engines(core, d)[share]
        return RemoteDMATransfer(dst_ids=[DstId(rid=rid, pnc=pid)], dma_engine_mask=sum(1 << x for x in e),
                                 remote_sem=T.sem["got%d" % j], src=a, dst=b), len(e)

    def send(j, q):
        k = len(topo.engines(core, T.cores[group[j][0]])) // 2
        calls = [[(0, codes, slice(0, k)), (1, codes, slice(k, None))] for codes in (True, False)]
        if group[j][1] == 1:
            calls = [[(0, True, slice(0, None, 2))], [(0, False, slice(1, None, 2))]]
        g.wait_ge(vs, q)
        count = 0
        for call in calls:
            tr = [transfer(j, *x) for x in call]
            g.remote_dma_fused([x for x, w in tr], local_sem=T.sem.sent)
            count += sum(w for x, w in tr)
        return count

    lefts = {(j, i): left(j, i) for j in range(NG + 1) for i in range(4)}
    sent = 0
    right(0, [0])
    for j in range(NG):
        full = right(j, [1, 2, 3])
        if j == NG - 1:
            V.wait_ge(T.sem.lpl, 256)
            places = v(V.tensor_scalar(T.offp[:], T.lp[:], 1, None, A.add))
        right(j + 1, [0])
        sent = sent + send(j, quantise(j, full))

    V.wait_ge(T.sem.luv, 32)
    quv = v(V.quantize_mx(T.quv[:], T.suv[:], T.uvt[:]))
    own = quantise(NG, right(NG, [1, 2, 3]))

    def products(bv, codes, scales, a, b, parts, last=False):
        cu = None
        for bk, c0, to in ((bv, 128, T.zv), (bv + 1, 0, T.zu)):
            z = t(PE.matmul_mx(bank(bk, b - a), T.quv[:, c0:c0 + 128], T.suv[:, c0:c0 + 128], codes[:, a:b], scales[:, a:b], True, True))
            for lo, j in parts:
                slot, w = CAPP * group[j][0], CAPP * group[j][1]
                src = T.ps[:, 512 * bk + lo - a:512 * bk + lo - a + w]
                if c0 or not last:
                    S.wait_ge(ts, z)
                    cv = s(S.activation(to[:, 1 + slot:1 + slot + w], src, F.Copy))
                else:
                    V.wait_ge(ts, z)
                    cu = v(V.tensor_copy(to[:, 1 + slot:1 + slot + w], src))
        return cv, cu

    PE.wait_ge(vs, quv)
    PE.wait_ge(ss, lefts[NG, 3])
    PE.wait_ge(T.sem.got0, 8)
    PE.wait_ge(T.sem.got1, 16)
    products(6, T.lc, T.ls, 0, land[2], [(land[0], 0), (land[1], 1)])
    PE.wait_ge(vs, own)
    products(4, T["q%d" % NG], T["s%d" % NG], 0, RUN, [(RUN - CAPP, NG)], True)
    PE.wait_ge(T.sem.got2, 16)
    products(0, T.lc, T.ls, land[3] - RUN, land[3], [(land[2], 2)], True)
    PE.wait_ge(T.sem.got3, 16)
    cv, cu = products(2, T.lc, T.ls, LAND - RUN, LAND, [(land[3], 3)], True)

    S.wait_ge(vs, places)
    S.wait_ge(ss, cv)
    V.wait_ge(vs, cu)
    V.wait_ge(ss, cv)
    parts, firsts = list(zip((0,) + CUT, CUT + (P,))), []
    for k, (a, b) in enumerate(parts):
        win = T.zv[:, 0:1 + SL].indirect(T.offp[:, a // 16:b // 16])
        firsts.append((vs, v(V.tensor_copy(T.first[:, a:b], win))) if k == 1 else (ss, s(S.activation(T.first[:, a:b], win, F.Copy))))
    done = []
    for (a, b), f in zip(parts, firsts):
        V.wait_ge(*f)
        done.append(v(V.tensor_tensor(T.yt[:, a:b], T.zu[:, 0:1 + SL].indirect(T.offp[:, 16 + a // 16:16 + b // 16]), T.first[:, a:b], A.add)))
    Y.wait_ge(vs, done[1])
    Y.dma_start(T.y[:, 0:CUT[1]], T.yt[:, 0:CUT[1]]).then_inc(T.sem.st0, 16)
    S.wait_ge(vs, done[2])
    S.dma_start(T.y[:, CUT[1]:P], T.yt[:, CUT[1]:P]).then_inc(T.sem.st1, 16)
    g.wait_ge(T.sem.sent, sent)
    Y.wait_ge(T.sem.st0, 16)
    S.wait_ge(T.sem.st1, 16)
